import numpy as np
import ml_dtypes


def mxq(x, axis, fmt="e4m3"):
    dtype, down = {"e4m3": (ml_dtypes.float8_e4m3fn, 7), "e5m2": (ml_dtypes.float8_e5m2, 14)}[fmt]
    v = np.moveaxis(np.asarray(x, np.float32).astype(ml_dtypes.bfloat16).astype(np.float64), axis, -1)
    blocks = v.reshape(v.shape[:-1] + (-1, 32))
    amax = np.abs(blocks).max(-1, keepdims=True)
    byte = np.maximum(np.where(amax > 0, np.frexp(amax)[1] - 1 + 127, 0) - down, 1)
    scale = np.exp2(byte - 127.0)
    codes = (blocks / scale).astype(np.float32).astype(dtype).astype(np.float64)
    return np.moveaxis((codes * scale).reshape(v.shape), -1, axis)


WIDE = False


def mx_kscale(k):
    if not WIDE:
        return np.ones(k)
    levels = np.array([10, -10, 5, -5, 0])
    if k % 512:
        return np.exp2(np.random.permutation(np.resize(levels, k // 32))).repeat(32)
    a = np.empty((k // 512, 16))
    for p in range(k // 512):
        a[p, :8] = np.random.permutation(np.resize(levels, 8))
        for g in range(8):
            far = levels[np.abs(levels - a[p, g]) >= 10]
            a[p, g + 8] = far[np.random.randint(len(far))]
    return np.exp2(a.ravel()).repeat(32)


def f64(x):
    return np.asarray(x).astype(np.float64)


def striped(idx):
    return np.tile(idx.reshape(-1, 16).T, (8, 1)).astype(np.uint16)


def unstriped(offs):
    return offs[:16].T.reshape(-1).astype(np.int64)


def pack_weight(w):
    k, n = w.shape
    w = f64(np.asarray(w, np.float32).astype(ml_dtypes.bfloat16)).reshape(k // 32, 32, n)
    amax = np.abs(w).max(1)
    byte = np.clip(np.where(amax > 0, np.frexp(amax)[1] - 1 + 127 - 7, 1), 1, 254)
    scaled = (w * np.exp2(127.0 - byte)[:, None, :]).reshape(k, n).astype(np.float32)
    words = np.ascontiguousarray(scaled.reshape(k // 512, 128, 4, n).transpose(0, 1, 3, 2)).astype(ml_dtypes.float8_e4m3fn).view(np.uint8)
    return words, np.ascontiguousarray(byte.astype(np.uint8).reshape(k // 512, 16, n))


def unpack_weight(words, scales):
    g, p, n, _ = words.shape
    vals = np.ascontiguousarray(words).view(ml_dtypes.float8_e4m3fn).astype(np.float64) * np.repeat(np.exp2(scales.astype(np.float64) - 127.0), 8, axis=1)[..., None]
    return vals.transpose(0, 1, 3, 2).reshape(g * 512, n)


def gelu(v):
    return 0.5 * v * (1.0 + np.tanh(np.sqrt(2.0 / np.pi) * (v + 0.044715 * v**3)))

def planes(y):
    n, m = y.shape
    v = y.astype(np.float32).astype(ml_dtypes.bfloat16).astype(np.float64).reshape(n // 32, 32, m)
    top = np.abs(v).max(1)
    byte = np.clip(np.where(top > 0, np.frexp(top)[1] - 1 + 127 - 7, 1), 1, 254)
    codes = (v * np.exp2(127.0 - byte)[:, None, :]).reshape(n, m).astype(np.float32).astype(ml_dtypes.float8_e4m3fn).view(np.uint8)
    words = codes.reshape(n // 512, 128, 4, m).transpose(0, 1, 3, 2)
    return np.ascontiguousarray(words), np.ascontiguousarray(byte.astype(np.uint8).reshape(n // 512, 16, m))


K, T, S, N, H = 512, 2048, 512, 512, 512


def setup_inputs():
    n = np.random.standard_normal
    s = mx_kscale(K)[:, None]
    u = mx_kscale(S)
    packed_xT = pack_weight(n((K, T)) * s)
    packed_w1 = pack_weight(n((S, N)) / np.sqrt(S) / u[:, None])
    return {
        "x_words": packed_xT[0],
        "x_scales": packed_xT[1],
        "wa": (n((K, H)) / np.sqrt(K) / s).astype(np.float32),
        "gt": (np.random.uniform(0.5, 1.5, (S, 1)) * u[:, None]).astype(np.float32),
        "w1_words": packed_w1[0],
        "w1_scales": packed_w1[1],
        "offs": striped(np.random.permutation(T)[:S]),
    }


def reference(x_words, x_scales, wa, gt, w1_words, w1_scales, offs):
    xq = unpack_weight(x_words, x_scales)[:, unstriped(offs)]
    y = xq.T @ mxq(f64(wa), 0, "e4m3")
    z = f64(gt) * gelu(y)
    out_0 = unpack_weight(w1_words, w1_scales).T @ mxq(z, 0, "e4m3")
    return (out_0,) + planes(out_0)

@@ -1,0 +1,181 @@
+from contextlib import ExitStack
+
+import concourse.mybir as mybir
+
+K, T, S, N, H = 512, 2048, 512, 512, 512
+FLOPS = 2 * S * K * H + 2 * N * S * H
+
+F32 = mybir.dt.float32
+BF16 = mybir.dt.bfloat16
+I32 = mybir.dt.int32
+U32 = mybir.dt.uint32
+U16 = mybir.dt.uint16
+U8 = mybir.dt.uint8
+FP8X4 = mybir.dt.float8_e4m3fn_x4
+GELU = mybir.ActivationFunctionType.Gelu_apprx_tanh
+MULT = mybir.AluOpType.mult
+
+P = 128
+PACK = 4
+W = 128
+CHUNKS = H // W
+WA_ON_VECTOR = [3]
+OUT_MODE = "VVSP"
+
+
+def tile_picked_tokmix_gelu_po_kernel(
+    tc, x_words, x_scales, wa, gt, w1_words, w1_scales, offs, out_0, out_1, out_2
+):
+    nc = tc.nc
+    with ExitStack() as ctx:
+        keep = ctx.enter_context(tc.tile_pool(name="keep", bufs=1))
+        psum = ctx.enter_context(tc.psum_pool(name="psum", bufs=1))
+
+        def tile(name, shape, dtype, tag=None):
+            return keep.tile(shape, dtype, name=name, tag=tag or name, align_bytes=64)
+
+        def load_scale_rows(queue, plane, rows):
+            for q in range(4):
+                queue[q % len(queue)].dma_start(out=plane[32 * q : 32 * q + 4, :].bitcast(I32), in_=rows[4 * q : 4 * q + 4, :].bitcast(I32))
+
+        def interleave(copy, dst, src):
+            copy(out=dst[:].rearrange("p (c i t) -> p c t i", i=4, t=PACK), in_=src.rearrange("p t (c i) -> p c t i", i=4))
+
+        wa_rows = wa.rearrange("(p t) n -> p t n", t=PACK)
+        out_rows = out_0.rearrange("(p t) n -> p t n", t=PACK)
+        out_words = out_1[0].rearrange("p n t -> p (n t)").bitcast(I32)
+        cols = [slice(c * W, (c + 1) * W) for c in range(CHUNKS)]
+
+        offsets = keep.tile([P, S // 16], U16, name="offsets")
+        nc.sync.dma_start(offsets[:], offs)
+
+        xs_table = tile("xs_table", [P, T], U8)
+        nc.vector.memset(xs_table[:, : T // 2].bitcast(I32), 0)
+        nc.gpsimd.memset(xs_table[:, T // 2 :].bitcast(I32), 0)
+        load_scale_rows([nc.scalar, nc.sync], xs_table, x_scales[0])
+        x_table = tile("x_table", [P, T], U32)
+        nc.sync.dma_start(out=x_table[:].bitcast(I32), in_=x_words[0].rearrange("p n t -> p (n t)").bitcast(I32))
+
+        wa_raw = []
+        for c in range(CHUNKS):
+            raw = tile("wa_raw%d" % c, [P, PACK, W], F32)
+            nc.sync.dma_start(out=raw[:], in_=wa_rows[:, :, cols[c]])
+            wa_raw.append(raw[:])
+
+        zero = tile("zero", [P, 1], F32)
+        nc.vector.memset(zero[:], 0.0)
+        bias = tile("bias", [P, 1], F32)
+        nc.scalar.activation(out=bias[:], in_=zero[:], func=GELU)
+
+        gate = tile("gate", [P, 1, PACK], F32)
+        nc.sync.dma_start(out=gate[:, 0, :], in_=gt.rearrange("(p t) o -> p (t o)", t=PACK))
+        w1s_raw = tile("w1s_raw", [P, N], U8)
+        nc.gpsimd.memset(w1s_raw[:].bitcast(I32), 0)
+        load_scale_rows([nc.scalar], w1s_raw, w1_scales[0])
+
+        xs_picked = tile("xs_picked", [P, S], U8)
+        nc.vector.tensor_copy(xs_picked[:], xs_table[:].indirect(offsets[:]))
+        xs_dealt = tile("xs_dealt", [P, S], U8)
+        nc.vector.tensor_copy(
+            out=xs_dealt[:].rearrange("p (t m) -> p t m", t=PACK), in_=xs_picked[:].rearrange("p (m t) -> p t m", t=PACK)
+        )
+        w1_raw = tile("w1_raw", [P, N], U32)
+        nc.sync.dma_start(out=w1_raw[:].bitcast(I32), in_=w1_words[0].rearrange("p n t -> p (n t)").bitcast(I32))
+
+        x_dealt = tile("x_dealt", [P, S], U32)
+        nc.vector.tensor_copy(x_dealt[:].rearrange("p (t m) -> p m t", t=PACK), x_table[:].indirect(offsets[:]))
+
+        def product(bank, codes, scales, rhs, rhs_scale):
+            for t in range(PACK):
+                m = slice(t * P, (t + 1) * P)
+                nc.tensor.matmul_mx(
+                    out=bank[:, t, :], lhsT=codes[:, m].bitcast(FP8X4), lhsT_scale=scales[:, m],
+                    rhs=rhs[:].bitcast(FP8X4), rhs_scale=rhs_scale[:], start=True, stop=True,
+                )
+
+        acts = {}
+        twin = {}
+
+        def project(c):
+            wb = tile("wa_bf%d" % c, [P, PACK * W], BF16)
+            interleave(nc.vector.tensor_copy if c in WA_ON_VECTOR else nc.scalar.copy, wb, wa_raw[c])
+            wq = tile("wa_q%d" % c, [P, W], U32)
+            ws = tile("wa_s%d" % c, [P, W], U8)
+            nc.vector.quantize_mx(out=wq[:].bitcast(FP8X4), scales=ws[:], in_=wb[:])
+            bank = psum.tile([P, PACK, W], F32, name="y%d" % c, tag="y%d" % c)
+            product(bank, x_dealt, xs_dealt, wq, ws)
+            acts[c] = bank
+
+        def activate(c):
+            g = tile("g%d" % c, [P, W, PACK], F32)
+            nc.scalar.activation(out=g[:], in_=acts[c][:].rearrange("p t n -> p n t"), func=GELU, bias=bias[:])
+            acts[c] = g
+
+        def weigh(c):
+            z = tile("z%d" % c, [P, W, PACK], BF16)
+            nc.vector.tensor_tensor(out=z[:], in0=acts[c][:], in1=gate[:].to_broadcast([P, W, PACK]), op=MULT)
+            acts[c] = z
+
+        def mix(c):
+            zq = tile("z_q%d" % c, [P, W], U32)
+            zs = tile("z_s%d" % c, [P, W], U8)
+            nc.vector.quantize_mx(out=zq[:].bitcast(FP8X4), scales=zs[:], in_=acts[c][:].rearrange("p n t -> p (n t)"))
+            if OUT_MODE[c] == "D":
+                twin[c] = psum.tile([P, PACK, W], F32, name="twin%d" % c, tag="y%d" % (CHUNKS - 1 - c))
+                product(twin[c], w1_dealt, w1s_dealt, zq, zs)
+            bank = psum.tile([P, PACK, W], F32, name="o%d" % c)
+            product(bank, w1_dealt, w1s_dealt, zq, zs)
+            acts[c] = bank
+
+        o_scales = tile("o_scales", [P, H], U8)
+        o_codes = tile("o_codes", [P, H], U32)
+
+        def leave(c):
+            res = tile("res%d" % c, [P, PACK, W], F32)
+            ob = tile("o_bf%d" % c, [P, PACK * W], BF16)
+            woven = ob[:].rearrange("p (n t) -> p n t", t=PACK)
+            if OUT_MODE[c] == "P":
+                nc.vector.tensor_copy(out=woven, in_=acts[c][:].rearrange("p t n -> p n t"))
+            if OUT_MODE[c] == "D":
+                nc.vector.tensor_copy(out=woven, in_=twin[c][:].rearrange("p t n -> p n t"))
+            nc.scalar.copy(out=res[:], in_=acts[c][:])
+            nc.sync.dma_start(out=out_rows[:, :, cols[c]], in_=res[:])
+            if OUT_MODE[c] == "S":
+                nc.scalar.copy(out=woven, in_=acts[c][:].rearrange("p t n -> p n t"))
+            if OUT_MODE[c] == "V":
+                interleave(nc.vector.tensor_copy, ob, res[:])
+            acts[c] = ob
+
+        def hand_on(c):
+            nc.vector.quantize_mx(out=o_codes[:, cols[c]].bitcast(FP8X4), scales=o_scales[:, cols[c]], in_=acts[c][:])
+            if c % 2:
+                pair = slice((c - 1) * W, (c + 1) * W)
+                nc.sync.dma_start(out=out_words[:, pair], in_=o_codes[:, pair].bitcast(I32))
+
+        project(0)
+        project(1)
+        project(2)
+        activate(0)
+        project(3)
+        w1s_dealt = tile("w1s_dealt", [P, N], U8, tag="wa_bf0")
+        nc.vector.tensor_copy(
+            out=w1s_dealt[:].rearrange("p (t m) -> p t m", t=PACK), in_=w1s_raw[:].rearrange("p (m t) -> p t m", t=PACK)
+        )
+        w1_dealt = tile("w1_dealt", [P, N], U32)
+        nc.vector.tensor_copy(
+            out=w1_dealt[:].rearrange("p (t m) -> p m t", t=PACK), in_=w1_raw[:].rearrange("p (m t) -> p m t", t=PACK)
+        )
+        weigh(0)
+        for c in range(1, CHUNKS):
+            activate(c)
+            weigh(c)
+            mix(c - 1)
+        mix(CHUNKS - 1)
+        for c in range(CHUNKS):
+            leave(c)
+            if c > 0:
+                hand_on(c - 1)
+        hand_on(CHUNKS - 1)
+        for q in range(4):
+            queue = nc.sync if q % 2 else nc.scalar
+            queue.dma_start(out=out_2[0][4 * q : 4 * q + 4, :].bitcast(I32), in_=o_scales[32 * q : 32 * q + 4, :].bitcast(I32))

@@ -19,8 +19,11 @@ P = 128
 PACK = 4
 W = 128
 CHUNKS = H // W
+X_HEAD = 512
+Z_REUSE = {}
+O_REUSE = {}
 WA_ON_VECTOR = [3]
-OUT_MODE = "VVSP"
+OUT_MODE = "SVVV"
 
 
 def tile_picked_tokmix_gelu_po_kernel(
@@ -46,6 +49,9 @@ def tile_picked_tokmix_gelu_po_kernel(
         out_words = out_1[0].rearrange("p n t -> p (n t)").bitcast(I32)
         cols = [slice(c * W, (c + 1) * W) for c in range(CHUNKS)]
 
+        x_rows = x_words[0].rearrange("p n t -> p (n t)").bitcast(I32)
+        x_table = tile("x_table", [P, T], U32)
+        nc.sync.dma_start(out=x_table[:, :X_HEAD].bitcast(I32), in_=x_rows[:, :X_HEAD])
         offsets = keep.tile([P, S // 16], U16, name="offsets")
         nc.sync.dma_start(offsets[:], offs)
 
@@ -53,25 +59,30 @@ def tile_picked_tokmix_gelu_po_kernel(
         nc.vector.memset(xs_table[:, : T // 2].bitcast(I32), 0)
         nc.gpsimd.memset(xs_table[:, T // 2 :].bitcast(I32), 0)
         load_scale_rows([nc.scalar, nc.sync], xs_table, x_scales[0])
-        x_table = tile("x_table", [P, T], U32)
-        nc.sync.dma_start(out=x_table[:].bitcast(I32), in_=x_words[0].rearrange("p n t -> p (n t)").bitcast(I32))
-
-        wa_raw = []
-        for c in range(CHUNKS):
-            raw = tile("wa_raw%d" % c, [P, PACK, W], F32)
-            nc.sync.dma_start(out=raw[:], in_=wa_rows[:, :, cols[c]])
-            wa_raw.append(raw[:])
+        nc.sync.dma_start(out=x_table[:, X_HEAD:].bitcast(I32), in_=x_rows[:, X_HEAD:])
 
         zero = tile("zero", [P, 1], F32)
         nc.vector.memset(zero[:], 0.0)
         bias = tile("bias", [P, 1], F32)
         nc.scalar.activation(out=bias[:], in_=zero[:], func=GELU)
 
-        gate = tile("gate", [P, 1, PACK], F32)
-        nc.sync.dma_start(out=gate[:, 0, :], in_=gt.rearrange("(p t) o -> p (t o)", t=PACK))
+        wa_raw = []
+
+        def load_wa(c):
+            raw = tile("wa_raw%d" % c, [P, PACK, W], F32)
+            nc.sync.dma_start(out=raw[:], in_=wa_rows[:, :, cols[c]])
+            wa_raw.append(raw[:])
+
+        for c in range(CHUNKS - 1):
+            load_wa(c)
         w1s_raw = tile("w1s_raw", [P, N], U8)
         nc.gpsimd.memset(w1s_raw[:].bitcast(I32), 0)
-        load_scale_rows([nc.scalar], w1s_raw, w1_scales[0])
+        load_scale_rows([nc.sync], w1s_raw, w1_scales[0])
+        w1_raw = tile("w1_raw", [P, N], U32)
+        nc.sync.dma_start(out=w1_raw[:].bitcast(I32), in_=w1_words[0].rearrange("p n t -> p (n t)").bitcast(I32))
+        load_wa(CHUNKS - 1)
+        gate = tile("gate", [P, 1, PACK], F32)
+        nc.sync.dma_start(out=gate[:, 0, :], in_=gt.rearrange("(p t) o -> p (t o)", t=PACK))
 
         xs_picked = tile("xs_picked", [P, S], U8)
         nc.vector.tensor_copy(xs_picked[:], xs_table[:].indirect(offsets[:]))
@@ -79,8 +90,6 @@ def tile_picked_tokmix_gelu_po_kernel(
         nc.vector.tensor_copy(
             out=xs_dealt[:].rearrange("p (t m) -> p t m", t=PACK), in_=xs_picked[:].rearrange("p (m t) -> p t m", t=PACK)
         )
-        w1_raw = tile("w1_raw", [P, N], U32)
-        nc.sync.dma_start(out=w1_raw[:].bitcast(I32), in_=w1_words[0].rearrange("p n t -> p (n t)").bitcast(I32))
 
         x_dealt = tile("x_dealt", [P, S], U32)
         nc.vector.tensor_copy(x_dealt[:].rearrange("p (t m) -> p m t", t=PACK), x_table[:].indirect(offsets[:]))
@@ -94,10 +103,17 @@ def tile_picked_tokmix_gelu_po_kernel(
                 )
 
         acts = {}
+        stage = {}
+
+        def staged(name):
+            if name not in stage:
+                stage[name] = tile(name, [P, PACK * W], BF16)
+            return stage[name]
+
         twin = {}
 
         def project(c):
-            wb = tile("wa_bf%d" % c, [P, PACK * W], BF16)
+            wb = staged("wa_bf%d" % c)
             interleave(nc.vector.tensor_copy if c in WA_ON_VECTOR else nc.scalar.copy, wb, wa_raw[c])
             wq = tile("wa_q%d" % c, [P, W], U32)
             ws = tile("wa_s%d" % c, [P, W], U8)
@@ -112,14 +128,14 @@ def tile_picked_tokmix_gelu_po_kernel(
             acts[c] = g
 
         def weigh(c):
-            z = tile("z%d" % c, [P, W, PACK], BF16)
-            nc.vector.tensor_tensor(out=z[:], in0=acts[c][:], in1=gate[:].to_broadcast([P, W, PACK]), op=MULT)
+            z = staged(Z_REUSE.get(c, "z%d" % c))
+            nc.vector.tensor_tensor(out=z[:].rearrange("p (n t) -> p n t", t=PACK), in0=acts[c][:], in1=gate[:].to_broadcast([P, W, PACK]), op=MULT)
             acts[c] = z
 
         def mix(c):
             zq = tile("z_q%d" % c, [P, W], U32)
             zs = tile("z_s%d" % c, [P, W], U8)
-            nc.vector.quantize_mx(out=zq[:].bitcast(FP8X4), scales=zs[:], in_=acts[c][:].rearrange("p n t -> p (n t)"))
+            nc.vector.quantize_mx(out=zq[:].bitcast(FP8X4), scales=zs[:], in_=acts[c][:])
             if OUT_MODE[c] == "D":
                 twin[c] = psum.tile([P, PACK, W], F32, name="twin%d" % c, tag="y%d" % (CHUNKS - 1 - c))
                 product(twin[c], w1_dealt, w1s_dealt, zq, zs)
@@ -132,7 +148,7 @@ def tile_picked_tokmix_gelu_po_kernel(
 
         def leave(c):
             res = tile("res%d" % c, [P, PACK, W], F32)
-            ob = tile("o_bf%d" % c, [P, PACK * W], BF16)
+            ob = staged(O_REUSE.get(c, "o_bf%d" % c))
             woven = ob[:].rearrange("p (n t) -> p n t", t=PACK)
             if OUT_MODE[c] == "P":
                 nc.vector.tensor_copy(out=woven, in_=acts[c][:].rearrange("p t n -> p n t"))
@@ -148,16 +164,12 @@ def tile_picked_tokmix_gelu_po_kernel(
 
         def hand_on(c):
             nc.vector.quantize_mx(out=o_codes[:, cols[c]].bitcast(FP8X4), scales=o_scales[:, cols[c]], in_=acts[c][:])
-            if c % 2:
-                pair = slice((c - 1) * W, (c + 1) * W)
-                nc.sync.dma_start(out=out_words[:, pair], in_=o_codes[:, pair].bitcast(I32))
 
         project(0)
         project(1)
         project(2)
         activate(0)
-        project(3)
-        w1s_dealt = tile("w1s_dealt", [P, N], U8, tag="wa_bf0")
+        w1s_dealt = tile("w1s_dealt", [P, N], U8)
         nc.vector.tensor_copy(
             out=w1s_dealt[:].rearrange("p (t m) -> p t m", t=PACK), in_=w1s_raw[:].rearrange("p (m t) -> p t m", t=PACK)
         )
@@ -165,6 +177,7 @@ def tile_picked_tokmix_gelu_po_kernel(
         nc.vector.tensor_copy(
             out=w1_dealt[:].rearrange("p (t m) -> p m t", t=PACK), in_=w1_raw[:].rearrange("p (m t) -> p m t", t=PACK)
         )
+        project(3)
         weigh(0)
         for c in range(1, CHUNKS):
             activate(c)
@@ -176,6 +189,7 @@ def tile_picked_tokmix_gelu_po_kernel(
             if c > 0:
                 hand_on(c - 1)
         hand_on(CHUNKS - 1)
+        nc.sync.dma_start(out=out_words, in_=o_codes[:].bitcast(I32))
         for q in range(4):
             queue = nc.sync if q % 2 else nc.scalar
             queue.dma_start(out=out_2[0][4 * q : 4 * q + 4, :].bitcast(I32), in_=o_scales[32 * q : 32 * q + 4, :].bitcast(I32))

@@ -17,13 +17,11 @@ MULT = mybir.AluOpType.mult
 
 P = 128
 PACK = 4
+QUADRANTS = 4
+RUN = 4
 W = 128
 CHUNKS = H // W
-X_HEAD = 512
-Z_REUSE = {}
-O_REUSE = {}
-WA_ON_VECTOR = [3]
-OUT_MODE = "SVVV"
+LAST = CHUNKS - 1
 
 
 def tile_picked_tokmix_gelu_po_kernel(
@@ -31,165 +29,153 @@ def tile_picked_tokmix_gelu_po_kernel(
 ):
     nc = tc.nc
     with ExitStack() as ctx:
-        keep = ctx.enter_context(tc.tile_pool(name="keep", bufs=1))
+        sbuf = ctx.enter_context(tc.tile_pool(name="sbuf", bufs=1))
         psum = ctx.enter_context(tc.psum_pool(name="psum", bufs=1))
 
         def tile(name, shape, dtype, tag=None):
-            return keep.tile(shape, dtype, name=name, tag=tag or name, align_bytes=64)
+            return sbuf.tile(shape, dtype, name=name, tag=tag or name, align_bytes=64)
 
-        def load_scale_rows(queue, plane, rows):
-            for q in range(4):
-                queue[q % len(queue)].dma_start(out=plane[32 * q : 32 * q + 4, :].bitcast(I32), in_=rows[4 * q : 4 * q + 4, :].bitcast(I32))
+        def as_words(packed):
+            return packed[0].rearrange("p n t -> p (n t)").bitcast(I32)
 
-        def interleave(copy, dst, src):
-            copy(out=dst[:].rearrange("p (c i t) -> p c t i", i=4, t=PACK), in_=src.rearrange("p t (c i) -> p c t i", i=4))
+        def scale_rows(plane, rows, q):
+            return plane[32 * q : 32 * q + 4, :].bitcast(I32), rows[0][4 * q : 4 * q + 4, :].bitcast(I32)
 
+        def weave(copy, dst, src):
+            copy(
+                out=dst[:].rearrange("p (c i t) -> p c t i", i=RUN, t=PACK),
+                in_=src.rearrange("p t (c i) -> p c t i", i=RUN),
+            )
+
+        def deal_bytes(dst, src):
+            nc.vector.tensor_copy(
+                out=dst[:].rearrange("p (t m) -> p t m", t=PACK), in_=src[:].rearrange("p (m t) -> p t m", t=PACK)
+            )
+
+        def product(bank, codes, scales, rhs_codes, rhs_scales):
+            for t in range(PACK):
+                dealt = slice(t * P, (t + 1) * P)
+                nc.tensor.matmul_mx(
+                    out=bank[:, t, :],
+                    lhsT=codes[:, dealt].bitcast(FP8X4),
+                    lhsT_scale=scales[:, dealt],
+                    rhs=rhs_codes[:].bitcast(FP8X4),
+                    rhs_scale=rhs_scales[:],
+                    start=True,
+                    stop=True,
+                )
+
+        cols = [slice(c * W, (c + 1) * W) for c in range(CHUNKS)]
         wa_rows = wa.rearrange("(p t) n -> p t n", t=PACK)
         out_rows = out_0.rearrange("(p t) n -> p t n", t=PACK)
-        out_words = out_1[0].rearrange("p n t -> p (n t)").bitcast(I32)
-        cols = [slice(c * W, (c + 1) * W) for c in range(CHUNKS)]
 
-        x_rows = x_words[0].rearrange("p n t -> p (n t)").bitcast(I32)
-        x_table = tile("x_table", [P, T], U32)
-        nc.sync.dma_start(out=x_table[:, :X_HEAD].bitcast(I32), in_=x_rows[:, :X_HEAD])
-        offsets = keep.tile([P, S // 16], U16, name="offsets")
+        gelu_out = tile("gelu_out", [P, CHUNKS * PACK * W], F32)
+        wa_raw = [tile("wa_raw%d" % c, [P, PACK, W], F32)[:] for c in range(LAST)]
+        wa_raw.append(gelu_out[:].rearrange("p (t n) -> p t n", t=PACK)[:, :, :W])
+
+        nc.sync.dma_start(out=wa_raw[0], in_=wa_rows[:, :, cols[0]])
+        offsets = sbuf.tile([P, S // 16], U16, name="offsets")
         nc.sync.dma_start(offsets[:], offs)
 
         xs_table = tile("xs_table", [P, T], U8)
-        nc.vector.memset(xs_table[:, : T // 2].bitcast(I32), 0)
-        nc.gpsimd.memset(xs_table[:, T // 2 :].bitcast(I32), 0)
-        load_scale_rows([nc.scalar, nc.sync], xs_table, x_scales[0])
-        nc.sync.dma_start(out=x_table[:, X_HEAD:].bitcast(I32), in_=x_rows[:, X_HEAD:])
+        nc.vector.memset(xs_table[:].bitcast(I32), 0)
+        for q in range(QUADRANTS):
+            place, rows = scale_rows(xs_table, x_scales, q)
+            (nc.sync if q % 2 else nc.scalar).dma_start(out=place, in_=rows)
+        x_table = tile("x_table", [P, T], U32)
+        nc.sync.dma_start(out=x_table[:].bitcast(I32), in_=as_words(x_words))
 
         zero = tile("zero", [P, 1], F32)
         nc.vector.memset(zero[:], 0.0)
         bias = tile("bias", [P, 1], F32)
         nc.scalar.activation(out=bias[:], in_=zero[:], func=GELU)
 
-        wa_raw = []
-
-        def load_wa(c):
-            raw = tile("wa_raw%d" % c, [P, PACK, W], F32)
-            nc.sync.dma_start(out=raw[:], in_=wa_rows[:, :, cols[c]])
-            wa_raw.append(raw[:])
-
-        for c in range(CHUNKS - 1):
-            load_wa(c)
-        w1s_raw = tile("w1s_raw", [P, N], U8)
-        nc.gpsimd.memset(w1s_raw[:].bitcast(I32), 0)
-        load_scale_rows([nc.sync], w1s_raw, w1_scales[0])
+        for c in range(1, CHUNKS):
+            nc.sync.dma_start(out=wa_raw[c], in_=wa_rows[:, :, cols[c]])
         w1_raw = tile("w1_raw", [P, N], U32)
-        nc.sync.dma_start(out=w1_raw[:].bitcast(I32), in_=w1_words[0].rearrange("p n t -> p (n t)").bitcast(I32))
-        load_wa(CHUNKS - 1)
+        nc.sync.dma_start(out=w1_raw[:].bitcast(I32), in_=as_words(w1_words))
+        w1s_raw = tile("w1s_raw", [P, N], U8)
+        nc.vector.memset(w1s_raw[:].bitcast(I32), 0)
+        for q in range(QUADRANTS):
+            place, rows = scale_rows(w1s_raw, w1_scales, q)
+            nc.sync.dma_start(out=place, in_=rows)
         gate = tile("gate", [P, 1, PACK], F32)
         nc.sync.dma_start(out=gate[:, 0, :], in_=gt.rearrange("(p t) o -> p (t o)", t=PACK))
 
         xs_picked = tile("xs_picked", [P, S], U8)
         nc.vector.tensor_copy(xs_picked[:], xs_table[:].indirect(offsets[:]))
         xs_dealt = tile("xs_dealt", [P, S], U8)
-        nc.vector.tensor_copy(
-            out=xs_dealt[:].rearrange("p (t m) -> p t m", t=PACK), in_=xs_picked[:].rearrange("p (m t) -> p t m", t=PACK)
-        )
-
+        deal_bytes(xs_dealt, xs_picked)
         x_dealt = tile("x_dealt", [P, S], U32)
         nc.vector.tensor_copy(x_dealt[:].rearrange("p (t m) -> p m t", t=PACK), x_table[:].indirect(offsets[:]))
 
-        def product(bank, codes, scales, rhs, rhs_scale):
-            for t in range(PACK):
-                m = slice(t * P, (t + 1) * P)
-                nc.tensor.matmul_mx(
-                    out=bank[:, t, :], lhsT=codes[:, m].bitcast(FP8X4), lhsT_scale=scales[:, m],
-                    rhs=rhs[:].bitcast(FP8X4), rhs_scale=rhs_scale[:], start=True, stop=True,
-                )
+        y_banks = []
+        for c in range(CHUNKS):
+            wa_bf = tile("wa_bf%d" % c, [P, PACK * W], BF16)
+            weave(nc.scalar.copy, wa_bf, wa_raw[c])
+            wa_codes = tile("wa_codes%d" % c, [P, W], U32, tag="xs_table" if c == 0 else None)
+            wa_scales = tile("wa_scales%d" % c, [P, W], U8)
+            nc.vector.quantize_mx(out=wa_codes[:].bitcast(FP8X4), scales=wa_scales[:], in_=wa_bf[:])
+            y_bank = psum.tile([P, PACK, W], F32, name="y_bank%d" % c)
+            product(y_bank, x_dealt, xs_dealt, wa_codes, wa_scales)
+            y_banks.append(y_bank)
 
-        acts = {}
-        stage = {}
-
-        def staged(name):
-            if name not in stage:
-                stage[name] = tile(name, [P, PACK * W], BF16)
-            return stage[name]
-
-        twin = {}
-
-        def project(c):
-            wb = staged("wa_bf%d" % c)
-            interleave(nc.vector.tensor_copy if c in WA_ON_VECTOR else nc.scalar.copy, wb, wa_raw[c])
-            wq = tile("wa_q%d" % c, [P, W], U32)
-            ws = tile("wa_s%d" % c, [P, W], U8)
-            nc.vector.quantize_mx(out=wq[:].bitcast(FP8X4), scales=ws[:], in_=wb[:])
-            bank = psum.tile([P, PACK, W], F32, name="y%d" % c, tag="y%d" % c)
-            product(bank, x_dealt, xs_dealt, wq, ws)
-            acts[c] = bank
-
-        def activate(c):
-            g = tile("g%d" % c, [P, W, PACK], F32)
-            nc.scalar.activation(out=g[:], in_=acts[c][:].rearrange("p t n -> p n t"), func=GELU, bias=bias[:])
-            acts[c] = g
-
-        def weigh(c):
-            z = staged(Z_REUSE.get(c, "z%d" % c))
-            nc.vector.tensor_tensor(out=z[:].rearrange("p (n t) -> p n t", t=PACK), in0=acts[c][:], in1=gate[:].to_broadcast([P, W, PACK]), op=MULT)
-            acts[c] = z
-
-        def mix(c):
-            zq = tile("z_q%d" % c, [P, W], U32)
-            zs = tile("z_s%d" % c, [P, W], U8)
-            nc.vector.quantize_mx(out=zq[:].bitcast(FP8X4), scales=zs[:], in_=acts[c][:])
-            if OUT_MODE[c] == "D":
-                twin[c] = psum.tile([P, PACK, W], F32, name="twin%d" % c, tag="y%d" % (CHUNKS - 1 - c))
-                product(twin[c], w1_dealt, w1s_dealt, zq, zs)
-            bank = psum.tile([P, PACK, W], F32, name="o%d" % c)
-            product(bank, w1_dealt, w1s_dealt, zq, zs)
-            acts[c] = bank
-
-        o_scales = tile("o_scales", [P, H], U8)
-        o_codes = tile("o_codes", [P, H], U32)
-
-        def leave(c):
-            res = tile("res%d" % c, [P, PACK, W], F32)
-            ob = staged(O_REUSE.get(c, "o_bf%d" % c))
-            woven = ob[:].rearrange("p (n t) -> p n t", t=PACK)
-            if OUT_MODE[c] == "P":
-                nc.vector.tensor_copy(out=woven, in_=acts[c][:].rearrange("p t n -> p n t"))
-            if OUT_MODE[c] == "D":
-                nc.vector.tensor_copy(out=woven, in_=twin[c][:].rearrange("p t n -> p n t"))
-            nc.scalar.copy(out=res[:], in_=acts[c][:])
-            nc.sync.dma_start(out=out_rows[:, :, cols[c]], in_=res[:])
-            if OUT_MODE[c] == "S":
-                nc.scalar.copy(out=woven, in_=acts[c][:].rearrange("p t n -> p n t"))
-            if OUT_MODE[c] == "V":
-                interleave(nc.vector.tensor_copy, ob, res[:])
-            acts[c] = ob
-
-        def hand_on(c):
-            nc.vector.quantize_mx(out=o_codes[:, cols[c]].bitcast(FP8X4), scales=o_scales[:, cols[c]], in_=acts[c][:])
-
-        project(0)
-        project(1)
-        project(2)
-        activate(0)
         w1s_dealt = tile("w1s_dealt", [P, N], U8)
-        nc.vector.tensor_copy(
-            out=w1s_dealt[:].rearrange("p (t m) -> p t m", t=PACK), in_=w1s_raw[:].rearrange("p (m t) -> p t m", t=PACK)
-        )
+        deal_bytes(w1s_dealt, w1s_raw)
         w1_dealt = tile("w1_dealt", [P, N], U32)
         nc.vector.tensor_copy(
-            out=w1_dealt[:].rearrange("p (t m) -> p m t", t=PACK), in_=w1_raw[:].rearrange("p (m t) -> p m t", t=PACK)
+            out=w1_dealt[:].rearrange("p (t c i) -> p c t i", t=PACK, i=RUN),
+            in_=w1_raw[:].rearrange("p (c i t) -> p c t i", t=PACK, i=RUN),
         )
-        project(3)
-        weigh(0)
+
+        def weigh(c):
+            g = gelu_out[:, c * PACK * W : (c + 1) * PACK * W].rearrange("p (n t) -> p n t", t=PACK)
+            nc.scalar.activation(out=g, in_=y_banks[c][:].rearrange("p t n -> p n t"), func=GELU, bias=bias[:])
+            z_bf = tile("z_bf%d" % c, [P, W, PACK], BF16)
+            nc.vector.tensor_tensor(out=z_bf[:], in0=g, in1=gate[:].to_broadcast([P, W, PACK]), op=MULT)
+            return z_bf
+
+        def mix(c, z_bf):
+            z_codes = tile("z_codes%d" % c, [P, W], U32)
+            z_scales = tile("z_scales%d" % c, [P, W], U8)
+            nc.vector.quantize_mx(
+                out=z_codes[:].bitcast(FP8X4), scales=z_scales[:], in_=z_bf[:].rearrange("p n t -> p (n t)")
+            )
+            out_bank = psum.tile([P, PACK, W], F32, name="out_bank%d" % c)
+            product(out_bank, w1_dealt, w1s_dealt, z_codes, z_scales)
+            return out_bank
+
+        def store_result(c, out_bank):
+            res = tile("res%d" % c, [P, PACK, W], F32)
+            nc.scalar.copy(out=res[:], in_=out_bank[:])
+            nc.sync.dma_start(out=out_rows[:, :, cols[c]], in_=res[:])
+            out_bf = tile("out_bf%d" % c, [P, PACK * W], BF16)
+            weave(nc.vector.tensor_copy, out_bf, res[:])
+            return out_bf
+
+        out_codes = tile("out_codes", [P, H], U32)
+        out_scales = tile("out_scales", [P, H], U8)
+
+        def quantise_result(c, out_bf):
+            nc.vector.quantize_mx(out=out_codes[:, cols[c]].bitcast(FP8X4), scales=out_scales[:, cols[c]], in_=out_bf[:])
+
+        def store_codes(span):
+            nc.sync.dma_start(out=as_words(out_1)[:, span], in_=out_codes[:, span].bitcast(I32))
+
+        z_bfs = [weigh(0)]
+        out_banks = []
         for c in range(1, CHUNKS):
-            activate(c)
-            weigh(c)
-            mix(c - 1)
-        mix(CHUNKS - 1)
-        for c in range(CHUNKS):
-            leave(c)
-            if c > 0:
-                hand_on(c - 1)
-        hand_on(CHUNKS - 1)
-        nc.sync.dma_start(out=out_words, in_=o_codes[:].bitcast(I32))
-        for q in range(4):
-            queue = nc.sync if q % 2 else nc.scalar
-            queue.dma_start(out=out_2[0][4 * q : 4 * q + 4, :].bitcast(I32), in_=o_scales[32 * q : 32 * q + 4, :].bitcast(I32))
+            z_bfs.append(weigh(c))
+            out_banks.append(mix(c - 1, z_bfs[c - 1]))
+        out_banks.append(mix(LAST, z_bfs[LAST]))
+
+        out_bfs = [store_result(0, out_banks[0])]
+        for c in range(1, CHUNKS):
+            out_bfs.append(store_result(c, out_banks[c]))
+            quantise_result(c - 1, out_bfs[c - 1])
+        store_codes(slice(0, LAST * W))
+        quantise_result(LAST, out_bfs[LAST])
+        store_codes(cols[LAST])
+        for q in range(QUADRANTS):
+            place, rows = scale_rows(out_scales, out_2, q)
+            (nc.sync if q % 2 else nc.scalar).dma_start(out=rows, in_=place)

@@ -19,6 +19,7 @@ P = 128
 PACK = 4
 QUADRANTS = 4
 RUN = 4
+PAIR = 2
 W = 128
 CHUNKS = H // W
 LAST = CHUNKS - 1
@@ -43,8 +44,8 @@ def tile_picked_tokmix_gelu_po_kernel(
 
         def weave(copy, dst, src):
             copy(
-                out=dst[:].rearrange("p (c i t) -> p c t i", i=RUN, t=PACK),
-                in_=src.rearrange("p t (c i) -> p c t i", i=RUN),
+                out=dst[:].rearrange("p (c i t) -> p c t i", i=PAIR, t=PACK),
+                in_=src.rearrange("p t (c i) -> p c t i", i=PAIR),
             )
 
         def deal_bytes(dst, src):
@@ -73,7 +74,8 @@ def tile_picked_tokmix_gelu_po_kernel(
         wa_raw = [tile("wa_raw%d" % c, [P, PACK, W], F32)[:] for c in range(LAST)]
         wa_raw.append(gelu_out[:].rearrange("p (t n) -> p t n", t=PACK)[:, :, :W])
 
-        nc.sync.dma_start(out=wa_raw[0], in_=wa_rows[:, :, cols[0]])
+        x_table = tile("x_table", [P, T], U32)
+        nc.sync.dma_start(out=x_table[:, :512].bitcast(I32), in_=as_words(x_words)[:, :512])
         offsets = sbuf.tile([P, S // 16], U16, name="offsets")
         nc.sync.dma_start(offsets[:], offs)
 
@@ -82,15 +84,14 @@ def tile_picked_tokmix_gelu_po_kernel(
         for q in range(QUADRANTS):
             place, rows = scale_rows(xs_table, x_scales, q)
             (nc.sync if q % 2 else nc.scalar).dma_start(out=place, in_=rows)
-        x_table = tile("x_table", [P, T], U32)
-        nc.sync.dma_start(out=x_table[:].bitcast(I32), in_=as_words(x_words))
+        nc.sync.dma_start(out=x_table[:, 512:].bitcast(I32), in_=as_words(x_words)[:, 512:])
 
         zero = tile("zero", [P, 1], F32)
         nc.vector.memset(zero[:], 0.0)
         bias = tile("bias", [P, 1], F32)
         nc.scalar.activation(out=bias[:], in_=zero[:], func=GELU)
 
-        for c in range(1, CHUNKS):
+        for c in range(0, CHUNKS):
             nc.sync.dma_start(out=wa_raw[c], in_=wa_rows[:, :, cols[c]])
         w1_raw = tile("w1_raw", [P, N], U32)
         nc.sync.dma_start(out=w1_raw[:].bitcast(I32), in_=as_words(w1_words))
@@ -113,7 +114,7 @@ def tile_picked_tokmix_gelu_po_kernel(
         for c in range(CHUNKS):
             wa_bf = tile("wa_bf%d" % c, [P, PACK * W], BF16)
             weave(nc.scalar.copy, wa_bf, wa_raw[c])
-            wa_codes = tile("wa_codes%d" % c, [P, W], U32, tag="xs_table" if c == 0 else None)
+            wa_codes = tile("wa_codes%d" % c, [P, W], U32)
             wa_scales = tile("wa_scales%d" % c, [P, W], U8)
             nc.vector.quantize_mx(out=wa_codes[:].bitcast(FP8X4), scales=wa_scales[:], in_=wa_bf[:])
             y_bank = psum.tile([P, PACK, W], F32, name="y_bank%d" % c)

@@ -23,6 +23,7 @@ PAIR = 2
 W = 128
 CHUNKS = H // W
 LAST = CHUNKS - 1
+X_HEAD = 512
 
 
 def tile_picked_tokmix_gelu_po_kernel(
@@ -33,8 +34,8 @@ def tile_picked_tokmix_gelu_po_kernel(
         sbuf = ctx.enter_context(tc.tile_pool(name="sbuf", bufs=1))
         psum = ctx.enter_context(tc.psum_pool(name="psum", bufs=1))
 
-        def tile(name, shape, dtype, tag=None):
-            return sbuf.tile(shape, dtype, name=name, tag=tag or name, align_bytes=64)
+        def tile(name, shape, dtype):
+            return sbuf.tile(shape, dtype, name=name, tag=name, align_bytes=64)
 
         def as_words(packed):
             return packed[0].rearrange("p n t -> p (n t)").bitcast(I32)
@@ -44,7 +45,7 @@ def tile_picked_tokmix_gelu_po_kernel(
 
         def weave(copy, dst, src):
             copy(
-                out=dst[:].rearrange("p (c i t) -> p c t i", i=PAIR, t=PACK),
+                out=dst.rearrange("p (c i t) -> p c t i", i=PAIR, t=PACK),
                 in_=src.rearrange("p t (c i) -> p c t i", i=PAIR),
             )
 
@@ -70,12 +71,8 @@ def tile_picked_tokmix_gelu_po_kernel(
         wa_rows = wa.rearrange("(p t) n -> p t n", t=PACK)
         out_rows = out_0.rearrange("(p t) n -> p t n", t=PACK)
 
-        gelu_out = tile("gelu_out", [P, CHUNKS * PACK * W], F32)
-        wa_raw = [tile("wa_raw%d" % c, [P, PACK, W], F32)[:] for c in range(LAST)]
-        wa_raw.append(gelu_out[:].rearrange("p (t n) -> p t n", t=PACK)[:, :, :W])
-
         x_table = tile("x_table", [P, T], U32)
-        nc.sync.dma_start(out=x_table[:, :512].bitcast(I32), in_=as_words(x_words)[:, :512])
+        nc.sync.dma_start(out=x_table[:, :X_HEAD].bitcast(I32), in_=as_words(x_words)[:, :X_HEAD])
         offsets = sbuf.tile([P, S // 16], U16, name="offsets")
         nc.sync.dma_start(offsets[:], offs)
 
@@ -84,15 +81,16 @@ def tile_picked_tokmix_gelu_po_kernel(
         for q in range(QUADRANTS):
             place, rows = scale_rows(xs_table, x_scales, q)
             (nc.sync if q % 2 else nc.scalar).dma_start(out=place, in_=rows)
-        nc.sync.dma_start(out=x_table[:, 512:].bitcast(I32), in_=as_words(x_words)[:, 512:])
+        nc.sync.dma_start(out=x_table[:, X_HEAD:].bitcast(I32), in_=as_words(x_words)[:, X_HEAD:])
 
         zero = tile("zero", [P, 1], F32)
         nc.vector.memset(zero[:], 0.0)
         bias = tile("bias", [P, 1], F32)
         nc.scalar.activation(out=bias[:], in_=zero[:], func=GELU)
 
-        for c in range(0, CHUNKS):
-            nc.sync.dma_start(out=wa_raw[c], in_=wa_rows[:, :, cols[c]])
+        wa_raw = [tile("wa_raw%d" % c, [P, PACK, W], F32) for c in range(CHUNKS)]
+        for c in range(CHUNKS):
+            nc.sync.dma_start(out=wa_raw[c][:], in_=wa_rows[:, :, cols[c]])
         w1_raw = tile("w1_raw", [P, N], U32)
         nc.sync.dma_start(out=w1_raw[:].bitcast(I32), in_=as_words(w1_words))
         w1s_raw = tile("w1s_raw", [P, N], U8)
@@ -113,7 +111,7 @@ def tile_picked_tokmix_gelu_po_kernel(
         y_banks = []
         for c in range(CHUNKS):
             wa_bf = tile("wa_bf%d" % c, [P, PACK * W], BF16)
-            weave(nc.scalar.copy, wa_bf, wa_raw[c])
+            weave(nc.vector.tensor_copy if c == LAST else nc.scalar.copy, wa_bf[:], wa_raw[c][:])
             wa_codes = tile("wa_codes%d" % c, [P, W], U32)
             wa_scales = tile("wa_scales%d" % c, [P, W], U8)
             nc.vector.quantize_mx(out=wa_codes[:].bitcast(FP8X4), scales=wa_scales[:], in_=wa_bf[:])
@@ -130,10 +128,10 @@ def tile_picked_tokmix_gelu_po_kernel(
         )
 
         def weigh(c):
-            g = gelu_out[:, c * PACK * W : (c + 1) * PACK * W].rearrange("p (n t) -> p n t", t=PACK)
-            nc.scalar.activation(out=g, in_=y_banks[c][:].rearrange("p t n -> p n t"), func=GELU, bias=bias[:])
+            g = tile("g%d" % c, [P, W, PACK], F32)
+            nc.scalar.activation(out=g[:], in_=y_banks[c][:].rearrange("p t n -> p n t"), func=GELU, bias=bias[:])
             z_bf = tile("z_bf%d" % c, [P, W, PACK], BF16)
-            nc.vector.tensor_tensor(out=z_bf[:], in0=g, in1=gate[:].to_broadcast([P, W, PACK]), op=MULT)
+            nc.vector.tensor_tensor(out=z_bf[:], in0=g[:], in1=gate[:].to_broadcast([P, W, PACK]), op=MULT)
             return z_bf
 
         def mix(c, z_bf):
@@ -148,10 +146,13 @@ def tile_picked_tokmix_gelu_po_kernel(
 
         def store_result(c, out_bank):
             res = tile("res%d" % c, [P, PACK, W], F32)
-            nc.scalar.copy(out=res[:], in_=out_bank[:])
-            nc.sync.dma_start(out=out_rows[:, :, cols[c]], in_=res[:])
             out_bf = tile("out_bf%d" % c, [P, PACK * W], BF16)
-            weave(nc.vector.tensor_copy, out_bf, res[:])
+            step = W // 2 if c == LAST else W
+            for n0 in range(0, W, step):
+                part = slice(n0, n0 + step)
+                nc.scalar.copy(out=res[:, :, part], in_=out_bank[:, :, part])
+                weave(nc.vector.tensor_copy, out_bf[:, PACK * n0 : PACK * (n0 + step)], res[:, :, part])
+            nc.sync.dma_start(out=out_rows[:, :, cols[c]], in_=res[:])
             return out_bf
 
         out_codes = tile("out_codes", [P, H], U32)

@@ -21,6 +21,8 @@ QUADRANTS = 4
 RUN = 4
 PAIR = 2
 W = 128
+HALF = W // 2
+SPREAD = 8
 CHUNKS = H // W
 LAST = CHUNKS - 1
 X_HEAD = 512
@@ -89,15 +91,15 @@ def tile_picked_tokmix_gelu_po_kernel(
         nc.scalar.activation(out=bias[:], in_=zero[:], func=GELU)
 
         wa_raw = [tile("wa_raw%d" % c, [P, PACK, W], F32) for c in range(CHUNKS)]
-        for c in range(CHUNKS):
+        for c in range(2):
+            nc.sync.dma_start(out=wa_raw[c][:], in_=wa_rows[:, :, cols[c]])
+        w1s_raw = tile("w1s_raw", [P, N], U8)
+        nc.vector.memset(w1s_raw[:].bitcast(I32), 0)
+        nc.sync.dma_start(out=w1s_raw[0:P:SPREAD, :].bitcast(I32), in_=w1_scales[0].bitcast(I32))
+        for c in range(2, CHUNKS):
             nc.sync.dma_start(out=wa_raw[c][:], in_=wa_rows[:, :, cols[c]])
         w1_raw = tile("w1_raw", [P, N], U32)
         nc.sync.dma_start(out=w1_raw[:].bitcast(I32), in_=as_words(w1_words))
-        w1s_raw = tile("w1s_raw", [P, N], U8)
-        nc.vector.memset(w1s_raw[:].bitcast(I32), 0)
-        for q in range(QUADRANTS):
-            place, rows = scale_rows(w1s_raw, w1_scales, q)
-            nc.sync.dma_start(out=place, in_=rows)
         gate = tile("gate", [P, 1, PACK], F32)
         nc.sync.dma_start(out=gate[:, 0, :], in_=gt.rearrange("(p t) o -> p (t o)", t=PACK))
 
@@ -107,6 +109,11 @@ def tile_picked_tokmix_gelu_po_kernel(
         deal_bytes(xs_dealt, xs_picked)
         x_dealt = tile("x_dealt", [P, S], U32)
         nc.vector.tensor_copy(x_dealt[:].rearrange("p (t m) -> p m t", t=PACK), x_table[:].indirect(offsets[:]))
+
+        w1s_dealt = tile("w1s_dealt", [P, N], U8)
+        deal_bytes(w1s_dealt, w1s_raw)
+        for s in range(1, 4):
+            nc.sync.dma_start(out=w1s_dealt[s:P:32, :].bitcast(I32), in_=w1s_dealt[SPREAD * s : P : 32, :].bitcast(I32))
 
         y_banks = []
         for c in range(CHUNKS):
@@ -119,20 +126,26 @@ def tile_picked_tokmix_gelu_po_kernel(
             product(y_bank, x_dealt, xs_dealt, wa_codes, wa_scales)
             y_banks.append(y_bank)
 
-        w1s_dealt = tile("w1s_dealt", [P, N], U8)
-        deal_bytes(w1s_dealt, w1s_raw)
         w1_dealt = tile("w1_dealt", [P, N], U32)
         nc.vector.tensor_copy(
             out=w1_dealt[:].rearrange("p (t c i) -> p c t i", t=PACK, i=RUN),
             in_=w1_raw[:].rearrange("p (c i t) -> p c t i", t=PACK, i=RUN),
         )
 
-        def weigh(c):
-            g = tile("g%d" % c, [P, W, PACK], F32)
-            nc.scalar.activation(out=g[:], in_=y_banks[c][:].rearrange("p t n -> p n t"), func=GELU, bias=bias[:])
-            z_bf = tile("z_bf%d" % c, [P, W, PACK], BF16)
-            nc.vector.tensor_tensor(out=z_bf[:], in0=g[:], in1=gate[:].to_broadcast([P, W, PACK]), op=MULT)
-            return z_bf
+        g = [
+            wa_raw[(c + 2) % CHUNKS][:].rearrange("p t n -> p (t n)").rearrange("p (n t) -> p n t", t=PACK)
+            for c in range(CHUNKS)
+        ]
+        z_bfs = [tile("z_bf%d" % c, [P, W, PACK], BF16) for c in range(CHUNKS)]
+
+        def weigh(c, half):
+            part = slice(half * HALF, (half + 1) * HALF)
+            nc.scalar.activation(
+                out=g[c][:, part, :], in_=y_banks[c][:, :, part].rearrange("p t n -> p n t"), func=GELU, bias=bias[:]
+            )
+            nc.vector.tensor_tensor(
+                out=z_bfs[c][:, part, :], in0=g[c][:, part, :], in1=gate[:].to_broadcast([P, HALF, PACK]), op=MULT
+            )
 
         def mix(c, z_bf):
             z_codes = tile("z_codes%d" % c, [P, W], U32)
@@ -164,11 +177,12 @@ def tile_picked_tokmix_gelu_po_kernel(
         def store_codes(span):
             nc.sync.dma_start(out=as_words(out_1)[:, span], in_=out_codes[:, span].bitcast(I32))
 
-        z_bfs = [weigh(0)]
         out_banks = []
-        for c in range(1, CHUNKS):
-            z_bfs.append(weigh(c))
-            out_banks.append(mix(c - 1, z_bfs[c - 1]))
+        for c in range(CHUNKS):
+            weigh(c, 0)
+            if c:
+                out_banks.append(mix(c - 1, z_bfs[c - 1]))
+            weigh(c, 1)
         out_banks.append(mix(LAST, z_bfs[LAST]))
 
         out_bfs = [store_result(0, out_banks[0])]

@@ -43,7 +43,7 @@ def tile_picked_tokmix_gelu_po_kernel(
             return packed[0].rearrange("p n t -> p (n t)").bitcast(I32)
 
         def scale_rows(plane, rows, q):
-            return plane[32 * q : 32 * q + 4, :].bitcast(I32), rows[0][4 * q : 4 * q + 4, :].bitcast(I32)
+            return plane[q:P:32, :].bitcast(I32), rows[0][q:16:4, :].bitcast(I32)
 
         def weave(copy, dst, src):
             copy(

@@ -25,7 +25,7 @@ HALF = W // 2
 SPREAD = 8
 CHUNKS = H // W
 LAST = CHUNKS - 1
-X_HEAD = 512
+X_HEAD = 384
 
 
 def tile_picked_tokmix_gelu_po_kernel(

@@ -103,10 +103,8 @@ def tile_picked_tokmix_gelu_po_kernel(
         gate = tile("gate", [P, 1, PACK], F32)
         nc.sync.dma_start(out=gate[:, 0, :], in_=gt.rearrange("(p t) o -> p (t o)", t=PACK))
 
-        xs_picked = tile("xs_picked", [P, S], U8)
-        nc.vector.tensor_copy(xs_picked[:], xs_table[:].indirect(offsets[:]))
         xs_dealt = tile("xs_dealt", [P, S], U8)
-        deal_bytes(xs_dealt, xs_picked)
+        nc.vector.tensor_copy(xs_dealt[:].rearrange("p (t m) -> p m t", t=PACK), xs_table[:].indirect(offsets[:]))
         x_dealt = tile("x_dealt", [P, S], U32)
         nc.vector.tensor_copy(x_dealt[:].rearrange("p (t m) -> p m t", t=PACK), x_table[:].indirect(offsets[:]))
 

@@ -25,7 +25,7 @@ HALF = W // 2
 SPREAD = 8
 CHUNKS = H // W
 LAST = CHUNKS - 1
-X_HEAD = 384
+X_HEAD = 448
 
 
 def tile_picked_tokmix_gelu_po_kernel(
@@ -56,11 +56,12 @@ def tile_picked_tokmix_gelu_po_kernel(
                 out=dst[:].rearrange("p (t m) -> p t m", t=PACK), in_=src[:].rearrange("p (m t) -> p t m", t=PACK)
             )
 
-        def product(bank, codes, scales, rhs_codes, rhs_scales):
+        def product(banks, codes, scales, rhs_codes, rhs_scales):
+            share = PACK // len(banks)
             for t in range(PACK):
                 dealt = slice(t * P, (t + 1) * P)
                 nc.tensor.matmul_mx(
-                    out=bank[:, t, :],
+                    out=banks[t // share][:, t % share, :],
                     lhsT=codes[:, dealt].bitcast(FP8X4),
                     lhsT_scale=scales[:, dealt],
                     rhs=rhs_codes[:].bitcast(FP8X4),
@@ -120,8 +121,8 @@ def tile_picked_tokmix_gelu_po_kernel(
             wa_codes = tile("wa_codes%d" % c, [P, W], U32)
             wa_scales = tile("wa_scales%d" % c, [P, W], U8)
             nc.vector.quantize_mx(out=wa_codes[:].bitcast(FP8X4), scales=wa_scales[:], in_=wa_bf[:])
-            y_bank = psum.tile([P, PACK, W], F32, name="y_bank%d" % c)
-            product(y_bank, x_dealt, xs_dealt, wa_codes, wa_scales)
+            y_bank = psum.tile([P, PACK, W], F32, name="y_bank%d" % c, tag="y_bank%d" % c)
+            product([y_bank], x_dealt, xs_dealt, wa_codes, wa_scales)
             y_banks.append(y_bank)
 
         w1_dealt = tile("w1_dealt", [P, N], U32)
@@ -151,17 +152,23 @@ def tile_picked_tokmix_gelu_po_kernel(
             nc.vector.quantize_mx(
                 out=z_codes[:].bitcast(FP8X4), scales=z_scales[:], in_=z_bf[:].rearrange("p n t -> p (n t)")
             )
-            out_bank = psum.tile([P, PACK, W], F32, name="out_bank%d" % c)
-            product(out_bank, w1_dealt, w1s_dealt, z_codes, z_scales)
-            return out_bank
+            if c == LAST:
+                banks = [psum.tile([P, 2, W], F32, name="pair_bank%d" % h, tag="y_bank%d" % h) for h in range(2)]
+            else:
+                banks = [psum.tile([P, PACK, W], F32, name="out_bank%d" % c)]
+            product(banks, w1_dealt, w1s_dealt, z_codes, z_scales)
+            return banks
 
-        def store_result(c, out_bank):
+        def store_result(c, banks):
             res = tile("res%d" % c, [P, PACK, W], F32)
             out_bf = tile("out_bf%d" % c, [P, PACK * W], BF16)
-            step = W // 2 if c == LAST else W
+            step = HALF if c == LAST else W
+            share = PACK // len(banks)
+            if c == LAST:
+                nc.scalar.copy(out=res[:, :share, :], in_=banks[0][:])
             for n0 in range(0, W, step):
                 part = slice(n0, n0 + step)
-                nc.scalar.copy(out=res[:, :, part], in_=out_bank[:, :, part])
+                nc.scalar.copy(out=res[:, PACK - share :, part], in_=banks[-1][:, :, part])
                 weave(nc.vector.tensor_copy, out_bf[:, PACK * n0 : PACK * (n0 + step)], res[:, :, part])
             nc.sync.dma_start(out=out_rows[:, :, cols[c]], in_=res[:])
             return out_bf

@@ -25,7 +25,7 @@ HALF = W // 2
 SPREAD = 8
 CHUNKS = H // W
 LAST = CHUNKS - 1
-X_HEAD = 448
+X_HEAD = 512
 
 
 def tile_picked_tokmix_gelu_po_kernel(
@@ -84,6 +84,9 @@ def tile_picked_tokmix_gelu_po_kernel(
         for q in range(QUADRANTS):
             place, rows = scale_rows(xs_table, x_scales, q)
             (nc.sync if q % 2 else nc.scalar).dma_start(out=place, in_=rows)
+        w1s_raw = tile("w1s_raw", [P, N], U8)
+        nc.vector.memset(w1s_raw[:].bitcast(I32), 0)
+        nc.sync.dma_start(out=w1s_raw[0:P:SPREAD, :].bitcast(I32), in_=w1_scales[0].bitcast(I32))
         nc.sync.dma_start(out=x_table[:, X_HEAD:].bitcast(I32), in_=as_words(x_words)[:, X_HEAD:])
 
         zero = tile("zero", [P, 1], F32)
@@ -92,12 +95,7 @@ def tile_picked_tokmix_gelu_po_kernel(
         nc.scalar.activation(out=bias[:], in_=zero[:], func=GELU)
 
         wa_raw = [tile("wa_raw%d" % c, [P, PACK, W], F32) for c in range(CHUNKS)]
-        for c in range(2):
-            nc.sync.dma_start(out=wa_raw[c][:], in_=wa_rows[:, :, cols[c]])
-        w1s_raw = tile("w1s_raw", [P, N], U8)
-        nc.vector.memset(w1s_raw[:].bitcast(I32), 0)
-        nc.sync.dma_start(out=w1s_raw[0:P:SPREAD, :].bitcast(I32), in_=w1_scales[0].bitcast(I32))
-        for c in range(2, CHUNKS):
+        for c in range(CHUNKS):
             nc.sync.dma_start(out=wa_raw[c][:], in_=wa_rows[:, :, cols[c]])
         w1_raw = tile("w1_raw", [P, N], U32)
         nc.sync.dma_start(out=w1_raw[:].bitcast(I32), in_=as_words(w1_words))
@@ -106,11 +104,11 @@ def tile_picked_tokmix_gelu_po_kernel(
 
         xs_dealt = tile("xs_dealt", [P, S], U8)
         nc.vector.tensor_copy(xs_dealt[:].rearrange("p (t m) -> p m t", t=PACK), xs_table[:].indirect(offsets[:]))
+        w1s_dealt = tile("w1s_dealt", [P, N], U8)
+        deal_bytes(w1s_dealt, w1s_raw)
         x_dealt = tile("x_dealt", [P, S], U32)
         nc.vector.tensor_copy(x_dealt[:].rearrange("p (t m) -> p m t", t=PACK), x_table[:].indirect(offsets[:]))
 
-        w1s_dealt = tile("w1s_dealt", [P, N], U8)
-        deal_bytes(w1s_dealt, w1s_raw)
         for s in range(1, 4):
             nc.sync.dma_start(out=w1s_dealt[s:P:32, :].bitcast(I32), in_=w1s_dealt[SPREAD * s : P : 32, :].bitcast(I32))
 
@@ -152,10 +150,8 @@ def tile_picked_tokmix_gelu_po_kernel(
             nc.vector.quantize_mx(
                 out=z_codes[:].bitcast(FP8X4), scales=z_scales[:], in_=z_bf[:].rearrange("p n t -> p (n t)")
             )
-            if c == LAST:
-                banks = [psum.tile([P, 2, W], F32, name="pair_bank%d" % h, tag="y_bank%d" % h) for h in range(2)]
-            else:
-                banks = [psum.tile([P, PACK, W], F32, name="out_bank%d" % c)]
+            tags = ["%s_bank%d" % ("out" if c < 2 else "y", 2 * (c % 2) + h) for h in range(2)]
+            banks = [psum.tile([P, 2, W], F32, name="pair%d_%d" % (c, h), tag=tags[h]) for h in range(2)]
             product(banks, w1_dealt, w1s_dealt, z_codes, z_scales)
             return banks
 
@@ -164,8 +160,7 @@ def tile_picked_tokmix_gelu_po_kernel(
             out_bf = tile("out_bf%d" % c, [P, PACK * W], BF16)
             step = HALF if c == LAST else W
             share = PACK // len(banks)
-            if c == LAST:
-                nc.scalar.copy(out=res[:, :share, :], in_=banks[0][:])
+            nc.scalar.copy(out=res[:, :share, :], in_=banks[0][:])
             for n0 in range(0, W, step):
                 part = slice(n0, n0 + step)
                 nc.scalar.copy(out=res[:, PACK - share :, part], in_=banks[-1][:, :, part])

@@ -25,7 +25,7 @@ HALF = W // 2
 SPREAD = 8
 CHUNKS = H // W
 LAST = CHUNKS - 1
-X_HEAD = 512
+X_HEAD = 768
 
 
 def tile_picked_tokmix_gelu_po_kernel(
@@ -83,10 +83,7 @@ def tile_picked_tokmix_gelu_po_kernel(
         nc.vector.memset(xs_table[:].bitcast(I32), 0)
         for q in range(QUADRANTS):
             place, rows = scale_rows(xs_table, x_scales, q)
-            (nc.sync if q % 2 else nc.scalar).dma_start(out=place, in_=rows)
-        w1s_raw = tile("w1s_raw", [P, N], U8)
-        nc.vector.memset(w1s_raw[:].bitcast(I32), 0)
-        nc.sync.dma_start(out=w1s_raw[0:P:SPREAD, :].bitcast(I32), in_=w1_scales[0].bitcast(I32))
+            nc.sync.dma_start(out=place, in_=rows)
         nc.sync.dma_start(out=x_table[:, X_HEAD:].bitcast(I32), in_=as_words(x_words)[:, X_HEAD:])
 
         zero = tile("zero", [P, 1], F32)
@@ -95,7 +92,12 @@ def tile_picked_tokmix_gelu_po_kernel(
         nc.scalar.activation(out=bias[:], in_=zero[:], func=GELU)
 
         wa_raw = [tile("wa_raw%d" % c, [P, PACK, W], F32) for c in range(CHUNKS)]
-        for c in range(CHUNKS):
+        for c in range(2):
+            nc.sync.dma_start(out=wa_raw[c][:], in_=wa_rows[:, :, cols[c]])
+        w1s_raw = tile("w1s_raw", [P, N], U8)
+        nc.vector.memset(w1s_raw[:].bitcast(I32), 0)
+        nc.sync.dma_start(out=w1s_raw[0:P:SPREAD, :].bitcast(I32), in_=w1_scales[0].bitcast(I32))
+        for c in range(2, CHUNKS):
             nc.sync.dma_start(out=wa_raw[c][:], in_=wa_rows[:, :, cols[c]])
         w1_raw = tile("w1_raw", [P, N], U32)
         nc.sync.dma_start(out=w1_raw[:].bitcast(I32), in_=as_words(w1_words))
@@ -104,11 +106,11 @@ def tile_picked_tokmix_gelu_po_kernel(
 
         xs_dealt = tile("xs_dealt", [P, S], U8)
         nc.vector.tensor_copy(xs_dealt[:].rearrange("p (t m) -> p m t", t=PACK), xs_table[:].indirect(offsets[:]))
-        w1s_dealt = tile("w1s_dealt", [P, N], U8)
-        deal_bytes(w1s_dealt, w1s_raw)
         x_dealt = tile("x_dealt", [P, S], U32)
         nc.vector.tensor_copy(x_dealt[:].rearrange("p (t m) -> p m t", t=PACK), x_table[:].indirect(offsets[:]))
 
+        w1s_dealt = tile("w1s_dealt", [P, N], U8)
+        deal_bytes(w1s_dealt, w1s_raw)
         for s in range(1, 4):
             nc.sync.dma_start(out=w1s_dealt[s:P:32, :].bitcast(I32), in_=w1s_dealt[SPREAD * s : P : 32, :].bitcast(I32))
 

@@ -163,11 +163,14 @@ def tile_picked_tokmix_gelu_po_kernel(
             step = HALF if c == LAST else W
             share = PACK // len(banks)
             nc.scalar.copy(out=res[:, :share, :], in_=banks[0][:])
+            sent = share if c == 0 else 0
+            if sent:
+                nc.sync.dma_start(out=out_rows[:, :sent, cols[c]], in_=res[:, :sent, :])
             for n0 in range(0, W, step):
                 part = slice(n0, n0 + step)
                 nc.scalar.copy(out=res[:, PACK - share :, part], in_=banks[-1][:, :, part])
                 weave(nc.vector.tensor_copy, out_bf[:, PACK * n0 : PACK * (n0 + step)], res[:, :, part])
-            nc.sync.dma_start(out=out_rows[:, :, cols[c]], in_=res[:])
+            nc.sync.dma_start(out=out_rows[:, sent:, cols[c]], in_=res[:, sent:, :])
             return out_bf
 
         out_codes = tile("out_codes", [P, H], U32)

@@ -25,7 +25,7 @@ HALF = W // 2
 SPREAD = 8
 CHUNKS = H // W
 LAST = CHUNKS - 1
-X_HEAD = 768
+X_HEAD = 896
 
 
 def tile_picked_tokmix_gelu_po_kernel(

@@ -64,8 +64,8 @@ def tile_picked_tokmix_gelu_po_kernel(
                     out=banks[t // share][:, t % share, :],
                     lhsT=codes[:, dealt].bitcast(FP8X4),
                     lhsT_scale=scales[:, dealt],
-                    rhs=rhs_codes[:].bitcast(FP8X4),
-                    rhs_scale=rhs_scales[:],
+                    rhs=rhs_codes.bitcast(FP8X4),
+                    rhs_scale=rhs_scales,
                     start=True,
                     stop=True,
                 )
@@ -122,7 +122,7 @@ def tile_picked_tokmix_gelu_po_kernel(
             wa_scales = tile("wa_scales%d" % c, [P, W], U8)
             nc.vector.quantize_mx(out=wa_codes[:].bitcast(FP8X4), scales=wa_scales[:], in_=wa_bf[:])
             y_bank = psum.tile([P, PACK, W], F32, name="y_bank%d" % c, tag="y_bank%d" % c)
-            product([y_bank], x_dealt, xs_dealt, wa_codes, wa_scales)
+            product([y_bank], x_dealt, xs_dealt, wa_codes[:], wa_scales[:])
             y_banks.append(y_bank)
 
         w1_dealt = tile("w1_dealt", [P, N], U32)
@@ -146,57 +146,69 @@ def tile_picked_tokmix_gelu_po_kernel(
                 out=z_bfs[c][:, part, :], in0=g[c][:, part, :], in1=gate[:].to_broadcast([P, HALF, PACK]), op=MULT
             )
 
-        def mix(c, z_bf):
-            z_codes = tile("z_codes%d" % c, [P, W], U32)
-            z_scales = tile("z_scales%d" % c, [P, W], U8)
+        def mix(name, z_bf, banks):
+            width = z_bf.shape[1]
+            z_codes = tile("z_codes" + name, [P, width], U32)
+            z_scales = tile("z_scales" + name, [P, width], U8)
             nc.vector.quantize_mx(
-                out=z_codes[:].bitcast(FP8X4), scales=z_scales[:], in_=z_bf[:].rearrange("p n t -> p (n t)")
+                out=z_codes[:].bitcast(FP8X4), scales=z_scales[:], in_=z_bf.rearrange("p n t -> p (n t)")
             )
-            tags = ["%s_bank%d" % ("out" if c < 2 else "y", 2 * (c % 2) + h) for h in range(2)]
-            banks = [psum.tile([P, 2, W], F32, name="pair%d_%d" % (c, h), tag=tags[h]) for h in range(2)]
-            product(banks, w1_dealt, w1s_dealt, z_codes, z_scales)
+            product(banks, w1_dealt, w1s_dealt, z_codes[:], z_scales[:])
             return banks
 
-        def store_result(c, banks):
-            res = tile("res%d" % c, [P, PACK, W], F32)
-            out_bf = tile("out_bf%d" % c, [P, PACK * W], BF16)
-            step = HALF if c == LAST else W
-            share = PACK // len(banks)
-            nc.scalar.copy(out=res[:, :share, :], in_=banks[0][:])
-            sent = share if c == 0 else 0
-            if sent:
-                nc.sync.dma_start(out=out_rows[:, :sent, cols[c]], in_=res[:, :sent, :])
-            for n0 in range(0, W, step):
-                part = slice(n0, n0 + step)
-                nc.scalar.copy(out=res[:, PACK - share :, part], in_=banks[-1][:, :, part])
-                weave(nc.vector.tensor_copy, out_bf[:, PACK * n0 : PACK * (n0 + step)], res[:, :, part])
-            nc.sync.dma_start(out=out_rows[:, sent:, cols[c]], in_=res[:, sent:, :])
-            return out_bf
+        out_tags = [("out_bank0", "out_bank1"), ("out_bank2", "out_bank3"), ("y_bank0", "y_bank1"), ("y_bank2", "y_bank3")]
+        halves = [slice(h * HALF, (h + 1) * HALF) for h in range(2)]
 
-        out_codes = tile("out_codes", [P, H], U32)
-        out_scales = tile("out_scales", [P, H], U8)
+        def mix_pairs(c):
+            banks = [psum.tile([P, 2, W], F32, name="pair%d_%d" % (c, h), tag=out_tags[c][h]) for h in range(2)]
+            return mix("%d" % c, z_bfs[c][:], banks)
 
-        def quantise_result(c, out_bf):
-            nc.vector.quantize_mx(out=out_codes[:, cols[c]].bitcast(FP8X4), scales=out_scales[:, cols[c]], in_=out_bf[:])
-
-        def store_codes(span):
-            nc.sync.dma_start(out=as_words(out_1)[:, span], in_=out_codes[:, span].bitcast(I32))
+        def mix_half(h):
+            banks = [psum.tile([P, PACK, HALF], F32, name="last%d" % h, tag=out_tags[LAST][h])]
+            return mix("last%d" % h, z_bfs[LAST][:, halves[h], :], banks)[0]
 
         out_banks = []
         for c in range(CHUNKS):
             weigh(c, 0)
             if c:
-                out_banks.append(mix(c - 1, z_bfs[c - 1]))
+                out_banks.append(mix_pairs(c - 1))
             weigh(c, 1)
-        out_banks.append(mix(LAST, z_bfs[LAST]))
+        last_banks = [mix_half(0)]
 
-        out_bfs = [store_result(0, out_banks[0])]
-        for c in range(1, CHUNKS):
-            out_bfs.append(store_result(c, out_banks[c]))
-            quantise_result(c - 1, out_bfs[c - 1])
-        store_codes(slice(0, LAST * W))
-        quantise_result(LAST, out_bfs[LAST])
-        store_codes(cols[LAST])
+        res = [tile("res%d" % c, [P, PACK, W], F32) for c in range(CHUNKS)]
+        out_bfs = [tile("out_bf%d" % c, [P, PACK * W], BF16) for c in range(CHUNKS)]
+        out_codes = tile("out_codes", [P, H], U32)
+        out_scales = tile("out_scales", [P, H], U8)
+
+        def leave(c):
+            for h in range(2):
+                nc.scalar.copy(out=res[c][:, 2 * h : 2 * h + 2, :], in_=out_banks[c][h][:])
+            nc.sync.dma_start(out=out_rows[:, :, cols[c]], in_=res[c][:])
+            weave(nc.vector.tensor_copy, out_bfs[c][:], res[c][:])
+
+        def quantise_result(c):
+            nc.vector.quantize_mx(
+                out=out_codes[:, cols[c]].bitcast(FP8X4), scales=out_scales[:, cols[c]], in_=out_bfs[c][:]
+            )
+
+        def store_codes(span):
+            nc.sync.dma_start(out=as_words(out_1)[:, span], in_=out_codes[:, span].bitcast(I32))
+
+        leave(0)
+        last_banks.append(mix_half(1))
+        leave(1)
+        quantise_result(0)
+        quantise_result(1)
+        store_codes(slice(0, 2 * W))
+        leave(2)
+        nc.scalar.copy(out=res[LAST][:, :, halves[0]], in_=last_banks[0][:])
+        weave(nc.vector.tensor_copy, out_bfs[LAST][:, : PACK * HALF], res[LAST][:, :, halves[0]])
+        quantise_result(2)
+        nc.scalar.copy(out=res[LAST][:, :, halves[1]], in_=last_banks[1][:])
+        nc.sync.dma_start(out=out_rows[:, :, cols[LAST]], in_=res[LAST][:])
+        weave(nc.scalar.copy, out_bfs[LAST][:, PACK * HALF :], last_banks[1][:])
+        quantise_result(LAST)
+        store_codes(slice(2 * W, H))
         for q in range(QUADRANTS):
             place, rows = scale_rows(out_scales, out_2, q)
             (nc.sync if q % 2 else nc.scalar).dma_start(out=rows, in_=place)

@@ -25,7 +25,8 @@ HALF = W // 2
 SPREAD = 8
 CHUNKS = H // W
 LAST = CHUNKS - 1
-X_HEAD = 896
+X_HEAD = 1024
+ROWS_AT = P - 16
 
 
 def tile_picked_tokmix_gelu_po_kernel(
@@ -64,8 +65,8 @@ def tile_picked_tokmix_gelu_po_kernel(
                     out=banks[t // share][:, t % share, :],
                     lhsT=codes[:, dealt].bitcast(FP8X4),
                     lhsT_scale=scales[:, dealt],
-                    rhs=rhs_codes.bitcast(FP8X4),
-                    rhs_scale=rhs_scales,
+                    rhs=rhs_codes[:].bitcast(FP8X4),
+                    rhs_scale=rhs_scales[:],
                     start=True,
                     stop=True,
                 )
@@ -74,16 +75,16 @@ def tile_picked_tokmix_gelu_po_kernel(
         wa_rows = wa.rearrange("(p t) n -> p t n", t=PACK)
         out_rows = out_0.rearrange("(p t) n -> p t n", t=PACK)
 
-        x_table = tile("x_table", [P, T], U32)
-        nc.sync.dma_start(out=x_table[:, :X_HEAD].bitcast(I32), in_=as_words(x_words)[:, :X_HEAD])
         offsets = sbuf.tile([P, S // 16], U16, name="offsets")
         nc.sync.dma_start(offsets[:], offs)
-
         xs_table = tile("xs_table", [P, T], U8)
-        nc.vector.memset(xs_table[:].bitcast(I32), 0)
-        for q in range(QUADRANTS):
-            place, rows = scale_rows(xs_table, x_scales, q)
-            nc.sync.dma_start(out=place, in_=rows)
+        nc.sync.dma_start(out=xs_table[ROWS_AT:, :].bitcast(I32), in_=x_scales[0].bitcast(I32))
+        nc.vector.memset(xs_table[:ROWS_AT, :].bitcast(I32), 0)
+        x_table = tile("x_table", [P, T], U32)
+        nc.sync.dma_start(out=x_table[:, :X_HEAD].bitcast(I32), in_=as_words(x_words)[:, :X_HEAD])
+        w1s_raw = tile("w1s_raw", [P, N], U8)
+        nc.vector.memset(w1s_raw[:].bitcast(I32), 0)
+        nc.sync.dma_start(out=w1s_raw[0:P:SPREAD, :].bitcast(I32), in_=w1_scales[0].bitcast(I32))
         nc.sync.dma_start(out=x_table[:, X_HEAD:].bitcast(I32), in_=as_words(x_words)[:, X_HEAD:])
 
         zero = tile("zero", [P, 1], F32)
@@ -94,20 +95,24 @@ def tile_picked_tokmix_gelu_po_kernel(
         wa_raw = [tile("wa_raw%d" % c, [P, PACK, W], F32) for c in range(CHUNKS)]
         for c in range(2):
             nc.sync.dma_start(out=wa_raw[c][:], in_=wa_rows[:, :, cols[c]])
-        w1s_raw = tile("w1s_raw", [P, N], U8)
-        nc.vector.memset(w1s_raw[:].bitcast(I32), 0)
-        nc.sync.dma_start(out=w1s_raw[0:P:SPREAD, :].bitcast(I32), in_=w1_scales[0].bitcast(I32))
+
+        xs_picked = tile("xs_picked", [P, S], U8)
+        nc.vector.tensor_copy(xs_picked[:].rearrange("p (t m) -> p m t", t=PACK), xs_table[:].indirect(offsets[:]))
+        xs_dealt = tile("xs_dealt", [P, S], U8)
+        nc.vector.memset(xs_dealt[:].bitcast(I32), 0)
+        for r in range(4):
+            nc.sync.dma_start(
+                out=xs_dealt[r:P:32, :].bitcast(I32), in_=xs_picked[ROWS_AT + r : P : 4, :].bitcast(I32)
+            )
+        x_dealt = tile("x_dealt", [P, S], U32)
+        nc.vector.tensor_copy(x_dealt[:].rearrange("p (t m) -> p m t", t=PACK), x_table[:].indirect(offsets[:]))
+
         for c in range(2, CHUNKS):
             nc.sync.dma_start(out=wa_raw[c][:], in_=wa_rows[:, :, cols[c]])
         w1_raw = tile("w1_raw", [P, N], U32)
         nc.sync.dma_start(out=w1_raw[:].bitcast(I32), in_=as_words(w1_words))
         gate = tile("gate", [P, 1, PACK], F32)
         nc.sync.dma_start(out=gate[:, 0, :], in_=gt.rearrange("(p t) o -> p (t o)", t=PACK))
-
-        xs_dealt = tile("xs_dealt", [P, S], U8)
-        nc.vector.tensor_copy(xs_dealt[:].rearrange("p (t m) -> p m t", t=PACK), xs_table[:].indirect(offsets[:]))
-        x_dealt = tile("x_dealt", [P, S], U32)
-        nc.vector.tensor_copy(x_dealt[:].rearrange("p (t m) -> p m t", t=PACK), x_table[:].indirect(offsets[:]))
 
         w1s_dealt = tile("w1s_dealt", [P, N], U8)
         deal_bytes(w1s_dealt, w1s_raw)
@@ -122,7 +127,7 @@ def tile_picked_tokmix_gelu_po_kernel(
             wa_scales = tile("wa_scales%d" % c, [P, W], U8)
             nc.vector.quantize_mx(out=wa_codes[:].bitcast(FP8X4), scales=wa_scales[:], in_=wa_bf[:])
             y_bank = psum.tile([P, PACK, W], F32, name="y_bank%d" % c, tag="y_bank%d" % c)
-            product([y_bank], x_dealt, xs_dealt, wa_codes[:], wa_scales[:])
+            product([y_bank], x_dealt, xs_dealt, wa_codes, wa_scales)
             y_banks.append(y_bank)
 
         w1_dealt = tile("w1_dealt", [P, N], U32)
@@ -146,69 +151,57 @@ def tile_picked_tokmix_gelu_po_kernel(
                 out=z_bfs[c][:, part, :], in0=g[c][:, part, :], in1=gate[:].to_broadcast([P, HALF, PACK]), op=MULT
             )
 
-        def mix(name, z_bf, banks):
-            width = z_bf.shape[1]
-            z_codes = tile("z_codes" + name, [P, width], U32)
-            z_scales = tile("z_scales" + name, [P, width], U8)
+        def mix(c, z_bf):
+            z_codes = tile("z_codes%d" % c, [P, W], U32)
+            z_scales = tile("z_scales%d" % c, [P, W], U8)
             nc.vector.quantize_mx(
-                out=z_codes[:].bitcast(FP8X4), scales=z_scales[:], in_=z_bf.rearrange("p n t -> p (n t)")
+                out=z_codes[:].bitcast(FP8X4), scales=z_scales[:], in_=z_bf[:].rearrange("p n t -> p (n t)")
             )
-            product(banks, w1_dealt, w1s_dealt, z_codes[:], z_scales[:])
+            tags = ["%s_bank%d" % ("out" if c < 2 else "y", 2 * (c % 2) + h) for h in range(2)]
+            banks = [psum.tile([P, 2, W], F32, name="pair%d_%d" % (c, h), tag=tags[h]) for h in range(2)]
+            product(banks, w1_dealt, w1s_dealt, z_codes, z_scales)
             return banks
 
-        out_tags = [("out_bank0", "out_bank1"), ("out_bank2", "out_bank3"), ("y_bank0", "y_bank1"), ("y_bank2", "y_bank3")]
-        halves = [slice(h * HALF, (h + 1) * HALF) for h in range(2)]
+        def store_result(c, banks):
+            res = tile("res%d" % c, [P, PACK, W], F32)
+            out_bf = tile("out_bf%d" % c, [P, PACK * W], BF16)
+            step = HALF if c == LAST else W
+            share = PACK // len(banks)
+            nc.scalar.copy(out=res[:, :share, :], in_=banks[0][:])
+            sent = share if c == 0 else 0
+            if sent:
+                nc.sync.dma_start(out=out_rows[:, :sent, cols[c]], in_=res[:, :sent, :])
+            for n0 in range(0, W, step):
+                part = slice(n0, n0 + step)
+                nc.scalar.copy(out=res[:, PACK - share :, part], in_=banks[-1][:, :, part])
+                weave(nc.vector.tensor_copy, out_bf[:, PACK * n0 : PACK * (n0 + step)], res[:, :, part])
+            nc.sync.dma_start(out=out_rows[:, sent:, cols[c]], in_=res[:, sent:, :])
+            return out_bf
 
-        def mix_pairs(c):
-            banks = [psum.tile([P, 2, W], F32, name="pair%d_%d" % (c, h), tag=out_tags[c][h]) for h in range(2)]
-            return mix("%d" % c, z_bfs[c][:], banks)
+        out_codes = tile("out_codes", [P, H], U32)
+        out_scales = tile("out_scales", [P, H], U8)
 
-        def mix_half(h):
-            banks = [psum.tile([P, PACK, HALF], F32, name="last%d" % h, tag=out_tags[LAST][h])]
-            return mix("last%d" % h, z_bfs[LAST][:, halves[h], :], banks)[0]
+        def quantise_result(c, out_bf):
+            nc.vector.quantize_mx(out=out_codes[:, cols[c]].bitcast(FP8X4), scales=out_scales[:, cols[c]], in_=out_bf[:])
+
+        def store_codes(span):
+            nc.sync.dma_start(out=as_words(out_1)[:, span], in_=out_codes[:, span].bitcast(I32))
 
         out_banks = []
         for c in range(CHUNKS):
             weigh(c, 0)
             if c:
-                out_banks.append(mix_pairs(c - 1))
+                out_banks.append(mix(c - 1, z_bfs[c - 1]))
             weigh(c, 1)
-        last_banks = [mix_half(0)]
+        out_banks.append(mix(LAST, z_bfs[LAST]))
 
-        res = [tile("res%d" % c, [P, PACK, W], F32) for c in range(CHUNKS)]
-        out_bfs = [tile("out_bf%d" % c, [P, PACK * W], BF16) for c in range(CHUNKS)]
-        out_codes = tile("out_codes", [P, H], U32)
-        out_scales = tile("out_scales", [P, H], U8)
-
-        def leave(c):
-            for h in range(2):
-                nc.scalar.copy(out=res[c][:, 2 * h : 2 * h + 2, :], in_=out_banks[c][h][:])
-            nc.sync.dma_start(out=out_rows[:, :, cols[c]], in_=res[c][:])
-            weave(nc.vector.tensor_copy, out_bfs[c][:], res[c][:])
-
-        def quantise_result(c):
-            nc.vector.quantize_mx(
-                out=out_codes[:, cols[c]].bitcast(FP8X4), scales=out_scales[:, cols[c]], in_=out_bfs[c][:]
-            )
-
-        def store_codes(span):
-            nc.sync.dma_start(out=as_words(out_1)[:, span], in_=out_codes[:, span].bitcast(I32))
-
-        leave(0)
-        last_banks.append(mix_half(1))
-        leave(1)
-        quantise_result(0)
-        quantise_result(1)
-        store_codes(slice(0, 2 * W))
-        leave(2)
-        nc.scalar.copy(out=res[LAST][:, :, halves[0]], in_=last_banks[0][:])
-        weave(nc.vector.tensor_copy, out_bfs[LAST][:, : PACK * HALF], res[LAST][:, :, halves[0]])
-        quantise_result(2)
-        nc.scalar.copy(out=res[LAST][:, :, halves[1]], in_=last_banks[1][:])
-        nc.sync.dma_start(out=out_rows[:, :, cols[LAST]], in_=res[LAST][:])
-        weave(nc.scalar.copy, out_bfs[LAST][:, PACK * HALF :], last_banks[1][:])
-        quantise_result(LAST)
-        store_codes(slice(2 * W, H))
+        out_bfs = [store_result(0, out_banks[0])]
+        for c in range(1, CHUNKS):
+            out_bfs.append(store_result(c, out_banks[c]))
+            quantise_result(c - 1, out_bfs[c - 1])
+        store_codes(slice(0, LAST * W))
+        quantise_result(LAST, out_bfs[LAST])
+        store_codes(cols[LAST])
         for q in range(QUADRANTS):
             place, rows = scale_rows(out_scales, out_2, q)
             (nc.sync if q % 2 else nc.scalar).dma_start(out=rows, in_=place)

@@ -77,15 +77,15 @@ def tile_picked_tokmix_gelu_po_kernel(
 
         offsets = sbuf.tile([P, S // 16], U16, name="offsets")
         nc.sync.dma_start(offsets[:], offs)
-        xs_table = tile("xs_table", [P, T], U8)
-        nc.sync.dma_start(out=xs_table[ROWS_AT:, :].bitcast(I32), in_=x_scales[0].bitcast(I32))
-        nc.vector.memset(xs_table[:ROWS_AT, :].bitcast(I32), 0)
         x_table = tile("x_table", [P, T], U32)
         nc.sync.dma_start(out=x_table[:, :X_HEAD].bitcast(I32), in_=as_words(x_words)[:, :X_HEAD])
-        w1s_raw = tile("w1s_raw", [P, N], U8)
-        nc.vector.memset(w1s_raw[:].bitcast(I32), 0)
-        nc.sync.dma_start(out=w1s_raw[0:P:SPREAD, :].bitcast(I32), in_=w1_scales[0].bitcast(I32))
         nc.sync.dma_start(out=x_table[:, X_HEAD:].bitcast(I32), in_=as_words(x_words)[:, X_HEAD:])
+        xs_table = tile("xs_table", [P, T], U8)
+        nc.scalar.dma_start(out=xs_table[ROWS_AT:, :].bitcast(I32), in_=x_scales[0].bitcast(I32))
+        w1s_raw = tile("w1s_raw", [P, N], U8)
+        nc.scalar.dma_start(out=w1s_raw[ROWS_AT:, :].bitcast(I32), in_=w1_scales[0].bitcast(I32))
+        nc.vector.memset(xs_table[:ROWS_AT, :].bitcast(I32), 0)
+        nc.vector.memset(w1s_raw[:ROWS_AT, :].bitcast(I32), 0)
 
         zero = tile("zero", [P, 1], F32)
         nc.vector.memset(zero[:], 0.0)
@@ -101,7 +101,7 @@ def tile_picked_tokmix_gelu_po_kernel(
         xs_dealt = tile("xs_dealt", [P, S], U8)
         nc.vector.memset(xs_dealt[:].bitcast(I32), 0)
         for r in range(4):
-            nc.sync.dma_start(
+            (nc.scalar if r % 2 else nc.sync).dma_start(
                 out=xs_dealt[r:P:32, :].bitcast(I32), in_=xs_picked[ROWS_AT + r : P : 4, :].bitcast(I32)
             )
         x_dealt = tile("x_dealt", [P, S], U32)
@@ -116,8 +116,10 @@ def tile_picked_tokmix_gelu_po_kernel(
 
         w1s_dealt = tile("w1s_dealt", [P, N], U8)
         deal_bytes(w1s_dealt, w1s_raw)
-        for s in range(1, 4):
-            nc.sync.dma_start(out=w1s_dealt[s:P:32, :].bitcast(I32), in_=w1s_dealt[SPREAD * s : P : 32, :].bitcast(I32))
+        for r in range(4):
+            nc.sync.dma_start(
+                out=w1s_dealt[r:P:32, :].bitcast(I32), in_=w1s_dealt[ROWS_AT + r : P : 4, :].bitcast(I32)
+            )
 
         y_banks = []
         for c in range(CHUNKS):

@@ -25,7 +25,7 @@ HALF = W // 2
 SPREAD = 8
 CHUNKS = H // W
 LAST = CHUNKS - 1
-X_HEAD = 1024
+W1_ROWS_AT = 64 - 16
 ROWS_AT = P - 16
 
 
@@ -75,17 +75,17 @@ def tile_picked_tokmix_gelu_po_kernel(
         wa_rows = wa.rearrange("(p t) n -> p t n", t=PACK)
         out_rows = out_0.rearrange("(p t) n -> p t n", t=PACK)
 
-        offsets = sbuf.tile([P, S // 16], U16, name="offsets")
-        nc.sync.dma_start(offsets[:], offs)
-        x_table = tile("x_table", [P, T], U32)
-        nc.sync.dma_start(out=x_table[:, :X_HEAD].bitcast(I32), in_=as_words(x_words)[:, :X_HEAD])
-        nc.sync.dma_start(out=x_table[:, X_HEAD:].bitcast(I32), in_=as_words(x_words)[:, X_HEAD:])
         xs_table = tile("xs_table", [P, T], U8)
         nc.scalar.dma_start(out=xs_table[ROWS_AT:, :].bitcast(I32), in_=x_scales[0].bitcast(I32))
+        offsets = sbuf.tile([P, S // 16], U16, name="offsets")
+        nc.sync.dma_start(offsets[:], offs)
         w1s_raw = tile("w1s_raw", [P, N], U8)
-        nc.scalar.dma_start(out=w1s_raw[ROWS_AT:, :].bitcast(I32), in_=w1_scales[0].bitcast(I32))
+        nc.scalar.dma_start(out=w1s_raw[W1_ROWS_AT:64, :].bitcast(I32), in_=w1_scales[0].bitcast(I32))
+        x_table = tile("x_table", [P, T], U32)
+        nc.sync.dma_start(out=x_table[:].bitcast(I32), in_=as_words(x_words))
         nc.vector.memset(xs_table[:ROWS_AT, :].bitcast(I32), 0)
-        nc.vector.memset(w1s_raw[:ROWS_AT, :].bitcast(I32), 0)
+        nc.vector.memset(w1s_raw[:W1_ROWS_AT, :].bitcast(I32), 0)
+        nc.vector.memset(w1s_raw[64:, :].bitcast(I32), 0)
 
         zero = tile("zero", [P, 1], F32)
         nc.vector.memset(zero[:], 0.0)
@@ -118,7 +118,7 @@ def tile_picked_tokmix_gelu_po_kernel(
         deal_bytes(w1s_dealt, w1s_raw)
         for r in range(4):
             nc.sync.dma_start(
-                out=w1s_dealt[r:P:32, :].bitcast(I32), in_=w1s_dealt[ROWS_AT + r : P : 4, :].bitcast(I32)
+                out=w1s_dealt[r:P:32, :].bitcast(I32), in_=w1s_dealt[W1_ROWS_AT + r : 64 : 4, :].bitcast(I32)
             )
 
         y_banks = []
@@ -147,7 +147,10 @@ def tile_picked_tokmix_gelu_po_kernel(
         def weigh(c, half):
             part = slice(half * HALF, (half + 1) * HALF)
             nc.scalar.activation(
-                out=g[c][:, part, :], in_=y_banks[c][:, :, part].rearrange("p t n -> p n t"), func=GELU, bias=bias[:]
+                out=g[c][:, part, :],
+                in_=y_banks[c][:, :, part].rearrange("p t n -> p n t"),
+                func=GELU,
+                bias=bias[:] if c == half == 0 else 0.0,
             )
             nc.vector.tensor_tensor(
                 out=z_bfs[c][:, part, :], in0=g[c][:, part, :], in1=gate[:].to_broadcast([P, HALF, PACK]), op=MULT

@@ -82,7 +82,9 @@ def tile_picked_tokmix_gelu_po_kernel(
         w1s_raw = tile("w1s_raw", [P, N], U8)
         nc.scalar.dma_start(out=w1s_raw[W1_ROWS_AT:64, :].bitcast(I32), in_=w1_scales[0].bitcast(I32))
         x_table = tile("x_table", [P, T], U32)
-        nc.sync.dma_start(out=x_table[:].bitcast(I32), in_=as_words(x_words))
+        for half in range(2):
+            span = slice(half * T // 2, (half + 1) * T // 2)
+            nc.sync.dma_start(out=x_table[:, span].bitcast(I32), in_=as_words(x_words)[:, span])
         nc.vector.memset(xs_table[:ROWS_AT, :].bitcast(I32), 0)
         nc.vector.memset(w1s_raw[:W1_ROWS_AT, :].bitcast(I32), 0)
         nc.vector.memset(w1s_raw[64:, :].bitcast(I32), 0)

@@ -175,7 +175,7 @@ def tile_picked_tokmix_gelu_po_kernel(
             step = HALF if c == LAST else W
             share = PACK // len(banks)
             nc.scalar.copy(out=res[:, :share, :], in_=banks[0][:])
-            sent = share if c == 0 else 0
+            sent = share if c < 2 else 0
             if sent:
                 nc.sync.dma_start(out=out_rows[:, :sent, cols[c]], in_=res[:, :sent, :])
             for n0 in range(0, W, step):

from contextlib import ExitStack

import concourse.mybir as mybir

K, T, S, N, H = 512, 2048, 512, 512, 512
FLOPS = 2 * S * K * H + 2 * N * S * H

F32 = mybir.dt.float32
BF16 = mybir.dt.bfloat16
I32 = mybir.dt.int32
U32 = mybir.dt.uint32
U16 = mybir.dt.uint16
U8 = mybir.dt.uint8
FP8X4 = mybir.dt.float8_e4m3fn_x4
GELU = mybir.ActivationFunctionType.Gelu_apprx_tanh
MULT = mybir.AluOpType.mult

P = 128
PACK = 4
QUADRANTS = 4
RUN = 4
PAIR = 2
W = 128
HALF = W // 2
SPREAD = 8
CHUNKS = H // W
LAST = CHUNKS - 1
W1_ROWS_AT = 64 - 16
ROWS_AT = P - 16


def tile_picked_tokmix_gelu_po_kernel(
    tc, x_words, x_scales, wa, gt, w1_words, w1_scales, offs, out_0, out_1, out_2
):
    nc = tc.nc
    with ExitStack() as ctx:
        sbuf = ctx.enter_context(tc.tile_pool(name="sbuf", bufs=1))
        psum = ctx.enter_context(tc.psum_pool(name="psum", bufs=1))

        def tile(name, shape, dtype):
            return sbuf.tile(shape, dtype, name=name, tag=name, align_bytes=64)

        def as_words(packed):
            return packed[0].rearrange("p n t -> p (n t)").bitcast(I32)

        def scale_rows(plane, rows, q):
            return plane[q:P:32, :].bitcast(I32), rows[0][q:16:4, :].bitcast(I32)

        def weave(copy, dst, src):
            copy(
                out=dst.rearrange("p (c i t) -> p c t i", i=PAIR, t=PACK),
                in_=src.rearrange("p t (c i) -> p c t i", i=PAIR),
            )

        def deal_bytes(dst, src):
            nc.vector.tensor_copy(
                out=dst[:].rearrange("p (t m) -> p t m", t=PACK), in_=src[:].rearrange("p (m t) -> p t m", t=PACK)
            )

        def product(banks, codes, scales, rhs_codes, rhs_scales):
            share = PACK // len(banks)
            for t in range(PACK):
                dealt = slice(t * P, (t + 1) * P)
                nc.tensor.matmul_mx(
                    out=banks[t // share][:, t % share, :],
                    lhsT=codes[:, dealt].bitcast(FP8X4),
                    lhsT_scale=scales[:, dealt],
                    rhs=rhs_codes[:].bitcast(FP8X4),
                    rhs_scale=rhs_scales[:],
                    start=True,
                    stop=True,
                )

        cols = [slice(c * W, (c + 1) * W) for c in range(CHUNKS)]
        wa_rows = wa.rearrange("(p t) n -> p t n", t=PACK)
        out_rows = out_0.rearrange("(p t) n -> p t n", t=PACK)

        xs_table = tile("xs_table", [P, T], U8)
        nc.scalar.dma_start(out=xs_table[ROWS_AT:, :].bitcast(I32), in_=x_scales[0].bitcast(I32))
        offsets = sbuf.tile([P, S // 16], U16, name="offsets")
        nc.sync.dma_start(offsets[:], offs)
        w1s_raw = tile("w1s_raw", [P, N], U8)
        nc.scalar.dma_start(out=w1s_raw[W1_ROWS_AT:64, :].bitcast(I32), in_=w1_scales[0].bitcast(I32))
        x_table = tile("x_table", [P, T], U32)
        for half in range(2):
            span = slice(half * T // 2, (half + 1) * T // 2)
            nc.sync.dma_start(out=x_table[:, span].bitcast(I32), in_=as_words(x_words)[:, span])
        nc.vector.memset(xs_table[:ROWS_AT, :].bitcast(I32), 0)
        nc.vector.memset(w1s_raw[:W1_ROWS_AT, :].bitcast(I32), 0)
        nc.vector.memset(w1s_raw[64:, :].bitcast(I32), 0)

        zero = tile("zero", [P, 1], F32)
        nc.vector.memset(zero[:], 0.0)
        bias = tile("bias", [P, 1], F32)
        nc.scalar.activation(out=bias[:], in_=zero[:], func=GELU)

        wa_raw = [tile("wa_raw%d" % c, [P, PACK, W], F32) for c in range(CHUNKS)]
        for c in range(2):
            nc.sync.dma_start(out=wa_raw[c][:], in_=wa_rows[:, :, cols[c]])

        xs_picked = tile("xs_picked", [P, S], U8)
        nc.vector.tensor_copy(xs_picked[:].rearrange("p (t m) -> p m t", t=PACK), xs_table[:].indirect(offsets[:]))
        xs_dealt = tile("xs_dealt", [P, S], U8)
        nc.vector.memset(xs_dealt[:].bitcast(I32), 0)
        for r in range(4):
            (nc.scalar if r % 2 else nc.sync).dma_start(
                out=xs_dealt[r:P:32, :].bitcast(I32), in_=xs_picked[ROWS_AT + r : P : 4, :].bitcast(I32)
            )
        x_dealt = tile("x_dealt", [P, S], U32)
        nc.vector.tensor_copy(x_dealt[:].rearrange("p (t m) -> p m t", t=PACK), x_table[:].indirect(offsets[:]))

        for c in range(2, CHUNKS):
            nc.sync.dma_start(out=wa_raw[c][:], in_=wa_rows[:, :, cols[c]])
        w1_raw = tile("w1_raw", [P, N], U32)
        nc.sync.dma_start(out=w1_raw[:].bitcast(I32), in_=as_words(w1_words))
        gate = tile("gate", [P, 1, PACK], F32)
        nc.sync.dma_start(out=gate[:, 0, :], in_=gt.rearrange("(p t) o -> p (t o)", t=PACK))

        w1s_dealt = tile("w1s_dealt", [P, N], U8)
        deal_bytes(w1s_dealt, w1s_raw)
        for r in range(4):
            nc.sync.dma_start(
                out=w1s_dealt[r:P:32, :].bitcast(I32), in_=w1s_dealt[W1_ROWS_AT + r : 64 : 4, :].bitcast(I32)
            )

        y_banks = []
        for c in range(CHUNKS):
            wa_bf = tile("wa_bf%d" % c, [P, PACK * W], BF16)
            weave(nc.vector.tensor_copy if c == LAST else nc.scalar.copy, wa_bf[:], wa_raw[c][:])
            wa_codes = tile("wa_codes%d" % c, [P, W], U32)
            wa_scales = tile("wa_scales%d" % c, [P, W], U8)
            nc.vector.quantize_mx(out=wa_codes[:].bitcast(FP8X4), scales=wa_scales[:], in_=wa_bf[:])
            y_bank = psum.tile([P, PACK, W], F32, name="y_bank%d" % c, tag="y_bank%d" % c)
            product([y_bank], x_dealt, xs_dealt, wa_codes, wa_scales)
            y_banks.append(y_bank)

        w1_dealt = tile("w1_dealt", [P, N], U32)
        nc.vector.tensor_copy(
            out=w1_dealt[:].rearrange("p (t c i) -> p c t i", t=PACK, i=RUN),
            in_=w1_raw[:].rearrange("p (c i t) -> p c t i", t=PACK, i=RUN),
        )

        g = [
            wa_raw[(c + 2) % CHUNKS][:].rearrange("p t n -> p (t n)").rearrange("p (n t) -> p n t", t=PACK)
            for c in range(CHUNKS)
        ]
        z_bfs = [tile("z_bf%d" % c, [P, W, PACK], BF16) for c in range(CHUNKS)]

        def weigh(c, half):
            part = slice(half * HALF, (half + 1) * HALF)
            nc.scalar.activation(
                out=g[c][:, part, :],
                in_=y_banks[c][:, :, part].rearrange("p t n -> p n t"),
                func=GELU,
                bias=bias[:] if c == half == 0 else 0.0,
            )
            nc.vector.tensor_tensor(
                out=z_bfs[c][:, part, :], in0=g[c][:, part, :], in1=gate[:].to_broadcast([P, HALF, PACK]), op=MULT
            )

        def mix(c, z_bf):
            z_codes = tile("z_codes%d" % c, [P, W], U32)
            z_scales = tile("z_scales%d" % c, [P, W], U8)
            nc.vector.quantize_mx(
                out=z_codes[:].bitcast(FP8X4), scales=z_scales[:], in_=z_bf[:].rearrange("p n t -> p (n t)")
            )
            tags = ["%s_bank%d" % ("out" if c < 2 else "y", 2 * (c % 2) + h) for h in range(2)]
            banks = [psum.tile([P, 2, W], F32, name="pair%d_%d" % (c, h), tag=tags[h]) for h in range(2)]
            product(banks, w1_dealt, w1s_dealt, z_codes, z_scales)
            return banks

        def store_result(c, banks):
            res = tile("res%d" % c, [P, PACK, W], F32)
            out_bf = tile("out_bf%d" % c, [P, PACK * W], BF16)
            step = HALF if c == LAST else W
            share = PACK // len(banks)
            nc.scalar.copy(out=res[:, :share, :], in_=banks[0][:])
            sent = share if c < 2 else 0
            if sent:
                nc.sync.dma_start(out=out_rows[:, :sent, cols[c]], in_=res[:, :sent, :])
            for n0 in range(0, W, step):
                part = slice(n0, n0 + step)
                nc.scalar.copy(out=res[:, PACK - share :, part], in_=banks[-1][:, :, part])
                weave(nc.vector.tensor_copy, out_bf[:, PACK * n0 : PACK * (n0 + step)], res[:, :, part])
            nc.sync.dma_start(out=out_rows[:, sent:, cols[c]], in_=res[:, sent:, :])
            return out_bf

        out_codes = tile("out_codes", [P, H], U32)
        out_scales = tile("out_scales", [P, H], U8)

        def quantise_result(c, out_bf):
            nc.vector.quantize_mx(out=out_codes[:, cols[c]].bitcast(FP8X4), scales=out_scales[:, cols[c]], in_=out_bf[:])

        def store_codes(span):
            nc.sync.dma_start(out=as_words(out_1)[:, span], in_=out_codes[:, span].bitcast(I32))

        out_banks = []
        for c in range(CHUNKS):
            weigh(c, 0)
            if c:
                out_banks.append(mix(c - 1, z_bfs[c - 1]))
            weigh(c, 1)
        out_banks.append(mix(LAST, z_bfs[LAST]))

        out_bfs = [store_result(0, out_banks[0])]
        for c in range(1, CHUNKS):
            out_bfs.append(store_result(c, out_banks[c]))
            quantise_result(c - 1, out_bfs[c - 1])
        store_codes(slice(0, LAST * W))
        quantise_result(LAST, out_bfs[LAST])
        store_codes(cols[LAST])
        for q in range(QUADRANTS):
            place, rows = scale_rows(out_scales, out_2, q)
            (nc.sync if q % 2 else nc.scalar).dma_start(out=rows, in_=place)
